import numpy as np
import ml_dtypes


def mxq(x, axis, fmt="e4m3"):
    dtype, down = {"e4m3": (ml_dtypes.float8_e4m3fn, 7), "e5m2": (ml_dtypes.float8_e5m2, 14)}[fmt]
    v = np.moveaxis(np.asarray(x, np.float32).astype(ml_dtypes.bfloat16).astype(np.float64), axis, -1)
    blocks = v.reshape(v.shape[:-1] + (-1, 32))
    amax = np.abs(blocks).max(-1, keepdims=True)
    byte = np.maximum(np.where(amax > 0, np.frexp(amax)[1] - 1 + 127, 0) - down, 1)
    scale = np.exp2(byte - 127.0)
    codes = (blocks / scale).astype(np.float32).astype(dtype).astype(np.float64)
    return np.moveaxis((codes * scale).reshape(v.shape), -1, axis)


WIDE = False


def mx_kscale(k):
    if not WIDE:
        return np.ones(k)
    levels = np.array([10, -10, 5, -5, 0])
    if k % 512:
        return np.exp2(np.random.permutation(np.resize(levels, k // 32))).repeat(32)
    a = np.empty((k // 512, 16))
    for p in range(k // 512):
        a[p, :8] = np.random.permutation(np.resize(levels, 8))
        for g in range(8):
            far = levels[np.abs(levels - a[p, g]) >= 10]
            a[p, g + 8] = far[np.random.randint(len(far))]
    return np.exp2(a.ravel()).repeat(32)


def f64(x):
    return np.asarray(x).astype(np.float64)


def striped(idx):
    return np.tile(idx.reshape(-1, 16).T, (8, 1)).astype(np.uint16)


def unstriped(offs):
    return offs[:16].T.reshape(-1).astype(np.int64)


E2M1 = np.array([0.0, 0.5, 1.0, 1.5, 2.0, 3.0, 4.0, 6.0, -0.0, -0.5, -1.0, -1.5, -2.0, -3.0, -4.0, -6.0])


def pack_weight(w, fmt):
    k, n = w.shape
    w = f64(np.asarray(w, np.float32).astype(ml_dtypes.bfloat16)).reshape(k // 32, 32, n)
    amax = np.abs(w).max(1)
    if fmt == "e4m3":
        byte = np.frexp(amax)[1] - 1 + 127 - 7
    else:
        mant, ex = np.frexp(amax / 6.0)
        byte = np.where(mant > 0.5, ex, ex - 1) + 127
    byte = np.clip(np.where(amax > 0, byte, 1), 1, 254)
    scaled = (w * np.exp2(127.0 - byte)[:, None, :]).reshape(k, n).astype(np.float32)
    by_word = np.ascontiguousarray(scaled.reshape(k // 512, 128, 4, n).transpose(0, 1, 3, 2))
    if fmt == "e4m3":
        words = by_word.astype(ml_dtypes.float8_e4m3fn).view(np.uint8)
    else:
        c = by_word.astype(ml_dtypes.float4_e2m1fn).view(np.uint8) & 0xF
        words = (c[..., 0::2] | (c[..., 1::2] << 4)).reshape(k // 512, 128, 2 * n)
    return np.ascontiguousarray(words), np.ascontiguousarray(byte.astype(np.uint8).reshape(k // 512, 16, n))


def unpack_weight(words, scales, fmt):
    g, _, n = scales.shape
    words = np.ascontiguousarray(words).reshape(g, 128, n, -1)
    if fmt == "e4m3":
        vals = words.view(ml_dtypes.float8_e4m3fn).astype(np.float64)
    else:
        nib = np.empty((g, 128, n, 4), np.uint8)
        nib[..., 0::2] = words & 0xF
        nib[..., 1::2] = words >> 4
        vals = E2M1[nib]
    vals = vals * np.repeat(np.exp2(scales.astype(np.float64) - 127.0), 8, axis=1)[..., None]
    return vals.transpose(0, 1, 3, 2).reshape(g * 512, n)


def gelu(v):
    return 0.5 * v * (1.0 + np.tanh(np.sqrt(2.0 / np.pi) * (v + 0.044715 * v**3)))


K, T, E, C, H, N = 2048, 640, 6, 128, 512, 256
R = 4


def by_expert(wq, xq):
    return np.concatenate([wq[e].T @ xq[:, e * C:(e + 1) * C] for e in range(E)], axis=1)


def setup_inputs():
    n = np.random.standard_normal
    s = mx_kscale(K)[:, None]
    u = mx_kscale(H)
    slot_token = np.concatenate([r * (T // R) + np.random.permutation(T // R)[:C // R] for e in range(E) for r in range(R)])
    w1 = [pack_weight(m, "e2m1") for m in n((E, K, H)) / np.sqrt(K) / s[None] * u[None, None, :]]
    w2 = [pack_weight(m, "e2m1") for m in n((E, H, N)) / np.sqrt(H) / u[None, :, None]]
    return {
        "xT": (n((K, T)) * s).astype(np.float32),
        "w1_words": np.stack([m[0] for m in w1]),
        "w1_scales": np.stack([m[1] for m in w1]),
        "w2_words": np.stack([m[0] for m in w2]),
        "w2_scales": np.stack([m[1] for m in w2]),
        "offs": striped(slot_token),
    }


def reference(xT, w1_words, w1_scales, w2_words, w2_scales, offs):
    idx = unstriped(offs)
    w1 = np.stack([unpack_weight(w1_words[e], w1_scales[e], "e2m1") for e in range(E)])
    w2 = np.stack([unpack_weight(w2_words[e], w2_scales[e], "e2m1") for e in range(E)])
    xq = mxq(f64(xT)[:, idx], 0, "e4m3")
    h = gelu(by_expert(w1, xq))
    y = by_expert(w2, mxq(h, 0, "e4m3"))
    return y.reshape(N, E, R, C // R).transpose(0, 2, 1, 3).reshape(N, E * C)

@@ -1,0 +1,254 @@
+from contextlib import ExitStack
+
+import concourse.mybir as mybir
+from concourse.masks import make_identity
+
+F32 = mybir.dt.float32
+BF16 = mybir.dt.bfloat16
+U32 = mybir.dt.uint32
+I32 = mybir.dt.int32
+U16 = mybir.dt.uint16
+U8 = mybir.dt.uint8
+E4M3 = mybir.dt.float8_e4m3fn_x4
+E2M1 = mybir.dt.float4_e2m1fn_x4
+COPY = mybir.ActivationFunctionType.Copy
+GELU = mybir.ActivationFunctionType.Gelu_apprx_tanh
+
+P = 128
+K, T, E, C, H, N, R = 2048, 640, 6, 128, 512, 256, 4
+S = K // 512
+U = C // R
+GROUPS = ((0, 1, 2, 3), (4, 5))
+FLOPS = 2 * E * C * (K * H + H * N)
+
+
+def tile_moe_eps_mlp_gelu_kernel(tc, xT, w1_words, w1_scales, w2_words, w2_scales, offs, out):
+    nc = tc.nc
+    with ExitStack() as ctx:
+        keep = ctx.enter_context(tc.tile_pool(name="keep", bufs=1))
+        psum = ctx.enter_context(tc.psum_pool(name="psum", bufs=1))
+
+        offsets = keep.tile([P, E * C // 16], U16, name="offsets")
+        raw = [keep.tile([P, 4, T], F32, name=f"raw{s}", align_bytes=64) for s in range(S)]
+        rounded = [keep.tile([P, T, 4], BF16, name=f"rounded{s}", align_bytes=64) for s in range(S - 1)]
+        rounded_a = keep.tile([P, 512, 4], BF16, name="rounded_a", tag="ring_a", align_bytes=64)
+        rounded_b = keep.tile([P, T - 512, 4], BF16, name="rounded_b", tag="ring_b", align_bytes=64)
+        words = [keep.tile([P, T], U32, name=f"words{s}", align_bytes=64) for s in range(S)]
+        scales = [keep.tile([P, T], U8, name=f"scales{s}", align_bytes=64) for s in range(S)]
+        slot_words = {}
+        slot_scales = {}
+        w1w = [keep.tile([P, S, len(group), 2 * H], U8, name=f"w1w{g}", align_bytes=64) for g, group in enumerate(GROUPS)]
+        w1s = [keep.tile([P, len(group) * S, H], U8, name=f"w1s{g}", align_bytes=64) for g, group in enumerate(GROUPS)]
+        w2w = keep.tile([P, E, 2 * N], U8, name="w2w", align_bytes=64)
+        w2s = keep.tile([P, E, N], U8, name="w2s", align_bytes=64)
+        hidden = [keep.tile([P, H], BF16, name=f"hidden{e}", align_bytes=64) for e in range(E)]
+        hturned = [keep.tile([P, C, 4], BF16, name=f"hturned{e}", align_bytes=64) for e in range(E)]
+        hwords = [keep.tile([P, C], U32, name=f"hwords{e}", align_bytes=64) for e in range(E)]
+        hscales = [keep.tile([P, C], U8, name=f"hscales{e}", align_bytes=64) for e in range(E)]
+        result = keep.tile([P, 2, R, E, U], F32, name="result", align_bytes=64)
+        ident = keep.tile([P, P], F32, name="ident")
+        warm = keep.tile([P, 2], F32, name="warm")
+        bank = [psum.tile([P, H], F32, name=f"bank{e}") for e in range(E)]
+
+        nc.vector.memset(warm[:], 0.0)
+        nc.scalar.activation(warm[:, 1:2], warm[:, 0:1], GELU)
+        for g in range(2):
+            nc.vector.memset(w1s[g][:].rearrange("p a i -> p (a i)").bitcast(I32), 0)
+        nc.vector.memset(w2s[:].rearrange("p a i -> p (a i)").bitcast(I32), 0)
+        for g in range(2):
+            nc.vector.memset(w1w[g][:, :, 0, 0:4].bitcast(I32), 0)
+        nc.vector.memset(w2w[:, 0:5:4, 0:4].bitcast(I32), 0)
+        for s in range(S):
+            nc.gpsimd.memset(scales[s][:], 0)
+        make_identity(nc, ident[:])
+
+        def load_x(s, a, b):
+            nc.sync.dma_start(out=raw[s][:, :, a:b], in_=xT[512 * s : 512 * (s + 1), :].rearrange("(p j) w -> p j w", j=4)[:, :, a:b])
+
+        def load_w1s(g):
+            half = slice(GROUPS[g][0], GROUPS[g][-1] + 1)
+            for r in range(4):
+                nc.sync.dma_start(out=w1s[g][r:P:32].bitcast(I32), in_=w1_scales[half, :, r:16:4, :].rearrange("e s q i -> q (e s) i").bitcast(I32))
+
+        def load_w1(g, s):
+            half = slice(GROUPS[g][0], GROUPS[g][-1] + 1)
+            nc.sync.dma_start(out=w1w[g][:, s].bitcast(I32), in_=w1_words[half, s].rearrange("e p n -> p e n").bitcast(I32))
+
+        def load_w2(g):
+            half = slice(GROUPS[g][0], GROUPS[g][-1] + 1)
+            nc.sync.dma_start(out=w2w[:, half, :].bitcast(I32), in_=w2_words[half].rearrange("e s p n -> p (e s) n").bitcast(I32))
+
+        load_x(0, 0, T)
+        nc.sync.dma_start(offsets[:], offs)
+        for s in range(1, S):
+            load_x(s, 0, T)
+        load_w1s(0)
+        load_w1s(1)
+        for r in range(4):
+            nc.sync.dma_start(out=w2s[r:P:32].bitcast(I32), in_=w2_scales[:, :, r:16:4, :].rearrange("e s q n -> q (e s) n").bitcast(I32))
+        for g in range(2):
+            for s in range(S):
+                load_w1(g, s)
+        load_w2(0)
+        load_w2(1)
+
+        def rounded_view(s, a, b):
+            if s < S - 1:
+                return rounded[s][:, a:b, :]
+            return rounded_a[:, a:b, :] if b <= 512 else rounded_b[:, a - 512 : b - 512, :]
+
+        def cast(engine_copy, s, a, b):
+            engine_copy(
+                rounded_view(s, a, b).rearrange("p (c i) t -> p c t i", i=4),
+                raw[s][:, :, a:b].rearrange("p t (c i) -> p c t i", i=4),
+            )
+
+        def quantise(s, a, b):
+            nc.vector.quantize_mx(
+                out=words[s][:, a:b].bitcast(E4M3), scales=scales[s][:, a:b], in_=rounded_view(s, a, b).rearrange("p c t -> p (c t)")
+            )
+
+        def gather_tiles(key, width, ring=False):
+            slot_words[key] = keep.tile([P, width], U32, name="slot_words%d%d" % key, tag="ring_a" if ring else "slot_words%d%d" % key, align_bytes=64)
+            slot_scales[key] = keep.tile([P, width], U8, name="slot_scales%d%d" % key, tag="ring_b" if ring else "slot_scales%d%d" % key, align_bytes=64)
+
+        def gather_words(key, first, a, b):
+            nc.vector.tensor_copy(slot_words[key][:, a - first : b - first], words[key[0]][:].indirect(offsets[:, a // 16 : b // 16]))
+
+        def gather_scales(key, first, a, b):
+            nc.vector.tensor_copy(slot_scales[key][:, a - first : b - first], scales[key[0]][:].indirect(offsets[:, a // 16 : b // 16]))
+
+        def first_layer(e, order):
+            g = 0 if e in GROUPS[0] else 1
+            u = e - GROUPS[g][0]
+            for s in order:
+                key, v = ((s, 0), e) if s < 2 else ((s, g), u)
+                nc.tensor.matmul_mx(
+                    out=bank[e][:],
+                    lhsT=slot_words[key][:, C * v : C * (v + 1)].bitcast(E4M3),
+                    lhsT_scale=slot_scales[key][:, C * v : C * (v + 1)],
+                    rhs=w1w[g][:, s, u, :].bitcast(E2M1),
+                    rhs_scale=w1s[g][:, S * u + s, :],
+                    start=(s == 0),
+                    stop=(s == S - 1),
+                )
+
+        def activate(e):
+            nc.scalar.activation(
+                hidden[e][:].rearrange("r (u p d) -> r u p d", u=2, d=2), bank[e][:].rearrange("r (p u d) -> r u p d", u=2, d=2), GELU
+            )
+
+        def turn(e):
+            pairs = hidden[e][:].bitcast(F32)
+            for u in range(2):
+                nc.tensor.transpose(bank[e][:, C * u : C * (u + 1)], pairs[:, P * u : P * (u + 1)], ident[:])
+
+        def unload_turned(e):
+            nc.vector.tensor_copy(
+                hturned[e][:].rearrange("p c t -> p (c t)").bitcast(F32).rearrange("p (c u) -> p c u", u=2),
+                bank[e][:, 0 : 2 * C].rearrange("p (u c) -> p c u", u=2),
+            )
+
+        def requantise(e):
+            nc.vector.quantize_mx(out=hwords[e][:].bitcast(E4M3), scales=hscales[e][:], in_=hturned[e][:].rearrange("p c t -> p (c t)"))
+
+        def second_layer(e):
+            for v in range(2):
+                nc.tensor.matmul_mx(
+                    out=bank[e][:, 2 * C + C * v : 2 * C + C * (v + 1)],
+                    lhsT=w2w[:, e, 2 * P * v : 2 * P * (v + 1)].bitcast(E2M1),
+                    lhsT_scale=w2s[:, e, P * v : P * (v + 1)],
+                    rhs=hwords[e][:].bitcast(E4M3),
+                    rhs_scale=hscales[e][:],
+                    start=True,
+                    stop=True,
+                )
+
+        def unload_result(e):
+            (nc.vector.tensor_copy if e == E - 1 else nc.scalar.copy)(result[:, :, :, e, :], bank[e][:, 2 * C : 4 * C].rearrange("p (v m u) -> p v m u", v=2, m=R))
+
+        def store(a, b):
+            view = out.rearrange("(v p) (m e u) -> v p m e u", v=2, m=R, e=E)
+            for v in range(2):
+                nc.sync.dma_start(
+                    out=view[v][:, :, a:b, :].rearrange("p m e u -> p m (e u)"),
+                    in_=result[:, v, :, a:b, :].rearrange("p m e u -> p m (e u)"),
+                )
+
+        cast(nc.vector.tensor_copy, 0, 0, 384)
+        cast(nc.scalar.copy, 0, 384, 512)
+        cast(nc.scalar.copy, 0, 512, T)
+        quantise(0, 0, 512)
+        quantise(0, 512, T)
+        half = 3 * C
+        gather_tiles((0, 0), 6 * C)
+        gather_words((0, 0), 0, 0, half)
+        gather_words((0, 0), 0, half, 6 * C)
+        gather_scales((0, 0), 0, 0, half)
+        cast(nc.scalar.copy, 1, 0, 512)
+        cast(nc.scalar.copy, 1, 512, T)
+        quantise(1, 0, 512)
+        quantise(1, 512, T)
+        gather_scales((0, 0), 0, half, 6 * C)
+        gather_tiles((1, 0), 6 * C)
+        gather_words((1, 0), 0, 0, half)
+        gather_words((1, 0), 0, half, 6 * C)
+        gather_scales((1, 0), 0, 0, half)
+        cast(nc.scalar.copy, 2, 0, 512)
+        cast(nc.scalar.copy, 2, 512, T)
+        quantise(2, 0, 512)
+        quantise(2, 512, T)
+        gather_scales((1, 0), 0, half, 6 * C)
+        for s in (0, 1):
+            for e in GROUPS[0]:
+                first_layer(e, (s,))
+        gather_tiles((2, 0), 4 * C)
+        gather_words((2, 0), 0, 0, 2 * C)
+        gather_scales((2, 0), 0, 0, 2 * C)
+        gather_words((2, 0), 0, 2 * C, 4 * C)
+        cast(nc.scalar.copy, 3, 0, 512)
+        cast(nc.scalar.copy, 3, 512, T)
+        quantise(3, 0, 512)
+        quantise(3, 512, T)
+        gather_scales((2, 0), 0, 2 * C, 4 * C)
+        gather_tiles((3, 0), 4 * C)
+        for a in (0, 2 * C):
+            gather_words((3, 0), 0, a, a + 2 * C)
+            gather_scales((3, 0), 0, a, a + 2 * C)
+        for s in (2, 3):
+            gather_tiles((s, 1), 2 * C, ring=(s == 2))
+            gather_words((s, 1), 4 * C, 4 * C, 6 * C)
+            gather_scales((s, 1), 4 * C, 4 * C, 6 * C)
+        for s in (2, 3):
+            for e in GROUPS[0]:
+                first_layer(e, (s,))
+        for e in GROUPS[0]:
+            activate(e)
+        for e in GROUPS[0]:
+            turn(e)
+        for s in range(S):
+            for e in GROUPS[1]:
+                first_layer(e, (s,))
+        activate(4)
+        activate(5)
+        for e in GROUPS[0]:
+            unload_turned(e)
+            if e > 0:
+                requantise(e - 1)
+        requantise(3)
+        turn(4)
+        turn(5)
+        unload_turned(4)
+        unload_turned(5)
+        requantise(4)
+        requantise(5)
+        for e in range(4):
+            second_layer(e)
+        for e in range(4):
+            unload_result(e)
+        store(0, 4)
+        second_layer(4)
+        second_layer(5)
+        unload_result(4)
+        unload_result(5)
+        store(4, 6)

@@ -11,14 +11,15 @@ U16 = mybir.dt.uint16
 U8 = mybir.dt.uint8
 E4M3 = mybir.dt.float8_e4m3fn_x4
 E2M1 = mybir.dt.float4_e2m1fn_x4
-COPY = mybir.ActivationFunctionType.Copy
 GELU = mybir.ActivationFunctionType.Gelu_apprx_tanh
 
 P = 128
 K, T, E, C, H, N, R = 2048, 640, 6, 128, 512, 256, 4
 S = K // 512
 U = C // R
-GROUPS = ((0, 1, 2, 3), (4, 5))
+G = 3
+CUT = 384
+WIDE = 512
 FLOPS = 2 * E * C * (K * H + H * N)
 
 
@@ -28,79 +29,58 @@ def tile_moe_eps_mlp_gelu_kernel(tc, xT, w1_words, w1_scales, w2_words, w2_scale
         keep = ctx.enter_context(tc.tile_pool(name="keep", bufs=1))
         psum = ctx.enter_context(tc.psum_pool(name="psum", bufs=1))
 
+        def sbuf(shape, dtype, name, tag=None):
+            return keep.tile(shape, dtype, name=name, tag=tag or name, align_bytes=64)
+
         offsets = keep.tile([P, E * C // 16], U16, name="offsets")
-        raw = [keep.tile([P, 4, T], F32, name=f"raw{s}", align_bytes=64) for s in range(S)]
-        rounded = [keep.tile([P, T, 4], BF16, name=f"rounded{s}", align_bytes=64) for s in range(S - 1)]
-        rounded_a = keep.tile([P, 512, 4], BF16, name="rounded_a", tag="ring_a", align_bytes=64)
-        rounded_b = keep.tile([P, T - 512, 4], BF16, name="rounded_b", tag="ring_b", align_bytes=64)
-        words = [keep.tile([P, T], U32, name=f"words{s}", align_bytes=64) for s in range(S)]
-        scales = [keep.tile([P, T], U8, name=f"scales{s}", align_bytes=64) for s in range(S)]
-        slot_words = {}
-        slot_scales = {}
-        w1w = [keep.tile([P, S, len(group), 2 * H], U8, name=f"w1w{g}", align_bytes=64) for g, group in enumerate(GROUPS)]
-        w1s = [keep.tile([P, len(group) * S, H], U8, name=f"w1s{g}", align_bytes=64) for g, group in enumerate(GROUPS)]
-        w2w = keep.tile([P, E, 2 * N], U8, name="w2w", align_bytes=64)
-        w2s = keep.tile([P, E, N], U8, name="w2s", align_bytes=64)
-        hidden = [keep.tile([P, H], BF16, name=f"hidden{e}", align_bytes=64) for e in range(E)]
-        hturned = [keep.tile([P, C, 4], BF16, name=f"hturned{e}", align_bytes=64) for e in range(E)]
-        hwords = [keep.tile([P, C], U32, name=f"hwords{e}", align_bytes=64) for e in range(E)]
-        hscales = [keep.tile([P, C], U8, name=f"hscales{e}", align_bytes=64) for e in range(E)]
-        result = keep.tile([P, 2, R, E, U], F32, name="result", align_bytes=64)
+        raw = {}
+        rounded = {}
+        for s in range(S):
+            raw[s, 0] = sbuf([P, 4, CUT], F32, f"raw{s}a")
+            raw[s, 1] = sbuf([P, 4, T - CUT], F32, f"raw{s}b")
+            rounded[s, 0] = sbuf([P, WIDE, 4], BF16, f"rounded{s}a")
+            rounded[s, 1] = sbuf([P, T - WIDE, 4], BF16, f"rounded{s}b")
+        words = [sbuf([P, T], U32, f"words{s}") for s in range(S)]
+        scales = [sbuf([P, T], U8, f"scales{s}") for s in range(S)]
+        w1s_early = sbuf([P, G * S * H], U8, "w1s_early")
+        hidden = [sbuf([P, H], BF16, f"hidden{e}") for e in range(E)]
+        hturned = [sbuf([P, C, 4], BF16, f"hturned{e}") for e in range(E)]
+        hwords = [sbuf([P, C], U32, f"hwords{e}") for e in range(E)]
+        hscales = [sbuf([P, C], U8, f"hscales{e}") for e in range(E)]
+        result = sbuf([P, 2, R, E, U], F32, "result")
         ident = keep.tile([P, P], F32, name="ident")
         warm = keep.tile([P, 2], F32, name="warm")
         bank = [psum.tile([P, H], F32, name=f"bank{e}") for e in range(E)]
+        early_out = [psum.tile([P, H], F32, name=f"early_out{v}") for v in range(2)]
 
         nc.vector.memset(warm[:], 0.0)
         nc.scalar.activation(warm[:, 1:2], warm[:, 0:1], GELU)
-        for g in range(2):
-            nc.vector.memset(w1s[g][:].rearrange("p a i -> p (a i)").bitcast(I32), 0)
-        nc.vector.memset(w2s[:].rearrange("p a i -> p (a i)").bitcast(I32), 0)
-        for g in range(2):
-            nc.vector.memset(w1w[g][:, :, 0, 0:4].bitcast(I32), 0)
-        nc.vector.memset(w2w[:, 0:5:4, 0:4].bitcast(I32), 0)
+        nc.vector.memset(w1s_early[:].bitcast(I32), 0)
         for s in range(S):
-            nc.gpsimd.memset(scales[s][:], 0)
+            nc.vector.memset(scales[s][:].bitcast(I32), 0)
         make_identity(nc, ident[:])
 
-        def load_x(s, a, b):
-            nc.sync.dma_start(out=raw[s][:, :, a:b], in_=xT[512 * s : 512 * (s + 1), :].rearrange("(p j) w -> p j w", j=4)[:, :, a:b])
+        def load_x(s, part):
+            a, b = ((0, CUT), (CUT, T))[part]
+            nc.sync.dma_start(out=raw[s, part][:], in_=xT[512 * s : 512 * (s + 1), :].rearrange("(p j) w -> p j w", j=4)[:, :, a:b])
 
-        def load_w1s(g):
-            half = slice(GROUPS[g][0], GROUPS[g][-1] + 1)
+        def load_scale_rows(plane, rows, width):
             for r in range(4):
-                nc.sync.dma_start(out=w1s[g][r:P:32].bitcast(I32), in_=w1_scales[half, :, r:16:4, :].rearrange("e s q i -> q (e s) i").bitcast(I32))
+                nc.sync.dma_start(
+                    out=plane[r:P:32].bitcast(I32).rearrange("q (a i) -> q a i", i=width // 4),
+                    in_=rows[:, r:16:4, :].rearrange("a q i -> q a i").bitcast(I32),
+                )
 
-        def load_w1(g, s):
-            half = slice(GROUPS[g][0], GROUPS[g][-1] + 1)
-            nc.sync.dma_start(out=w1w[g][:, s].bitcast(I32), in_=w1_words[half, s].rearrange("e p n -> p e n").bitcast(I32))
-
-        def load_w2(g):
-            half = slice(GROUPS[g][0], GROUPS[g][-1] + 1)
-            nc.sync.dma_start(out=w2w[:, half, :].bitcast(I32), in_=w2_words[half].rearrange("e s p n -> p (e s) n").bitcast(I32))
-
-        load_x(0, 0, T)
-        nc.sync.dma_start(offsets[:], offs)
-        for s in range(1, S):
-            load_x(s, 0, T)
-        load_w1s(0)
-        load_w1s(1)
-        for r in range(4):
-            nc.sync.dma_start(out=w2s[r:P:32].bitcast(I32), in_=w2_scales[:, :, r:16:4, :].rearrange("e s q n -> q (e s) n").bitcast(I32))
-        for g in range(2):
-            for s in range(S):
-                load_w1(g, s)
-        load_w2(0)
-        load_w2(1)
+        def raw_view(s, a, b):
+            return raw[s, 0][:, :, a:b] if b <= CUT else raw[s, 1][:, :, a - CUT : b - CUT]
 
         def rounded_view(s, a, b):
-            if s < S - 1:
-                return rounded[s][:, a:b, :]
-            return rounded_a[:, a:b, :] if b <= 512 else rounded_b[:, a - 512 : b - 512, :]
+            return rounded[s, 0][:, a:b, :] if b <= WIDE else rounded[s, 1][:, a - WIDE : b - WIDE, :]
 
         def cast(engine_copy, s, a, b):
             engine_copy(
                 rounded_view(s, a, b).rearrange("p (c i) t -> p c t i", i=4),
-                raw[s][:, :, a:b].rearrange("p t (c i) -> p c t i", i=4),
+                raw_view(s, a, b).rearrange("p t (c i) -> p c t i", i=4),
             )
 
         def quantise(s, a, b):
@@ -108,147 +88,172 @@ def tile_moe_eps_mlp_gelu_kernel(tc, xT, w1_words, w1_scales, w2_words, w2_scale
                 out=words[s][:, a:b].bitcast(E4M3), scales=scales[s][:, a:b], in_=rounded_view(s, a, b).rearrange("p c t -> p (c t)")
             )
 
-        def gather_tiles(key, width, ring=False):
-            slot_words[key] = keep.tile([P, width], U32, name="slot_words%d%d" % key, tag="ring_a" if ring else "slot_words%d%d" % key, align_bytes=64)
-            slot_scales[key] = keep.tile([P, width], U8, name="slot_scales%d%d" % key, tag="ring_b" if ring else "slot_scales%d%d" % key, align_bytes=64)
+        def round_and_quantise(s):
+            cast(nc.scalar.copy, s, 0, CUT)
+            cast(nc.scalar.copy, s, CUT, WIDE)
+            cast(nc.scalar.copy, s, WIDE, T)
+            quantise(s, 0, WIDE)
+            quantise(s, WIDE, T)
 
-        def gather_words(key, first, a, b):
-            nc.vector.tensor_copy(slot_words[key][:, a - first : b - first], words[key[0]][:].indirect(offsets[:, a // 16 : b // 16]))
+        slot_words = {}
+        slot_scales = {}
 
-        def gather_scales(key, first, a, b):
-            nc.vector.tensor_copy(slot_scales[key][:, a - first : b - first], scales[key[0]][:].indirect(offsets[:, a // 16 : b // 16]))
+        def gather(dst, table, g, a=0, b=G * C):
+            first = G * C * g
+            nc.vector.tensor_copy(dst[:, a:b], table[:].indirect(offsets[:, (first + a) // 16 : (first + b) // 16]))
 
-        def first_layer(e, order):
-            g = 0 if e in GROUPS[0] else 1
-            u = e - GROUPS[g][0]
-            for s in order:
-                key, v = ((s, 0), e) if s < 2 else ((s, g), u)
+        def gather_words(s, g, tag=None, a=0, b=G * C):
+            if (s, g) not in slot_words:
+                slot_words[s, g] = sbuf([P, G * C], U32, f"slot_words{s}{g}", tag)[:]
+            gather(slot_words[s, g], words[s], g, a, b)
+
+        def gather_scales(s, g, tag=None, a=0, b=G * C):
+            if (s, g) not in slot_scales:
+                slot_scales[s, g] = sbuf([P, G * C], U8, f"slot_scales{s}{g}", tag)[:]
+            gather(slot_scales[s, g], scales[s], g, a, b)
+
+        w1_rows = w1_scales.rearrange("e s q i -> (e s) q i")
+
+        load_x(0, 0)
+        nc.sync.dma_start(offsets[:], offs)
+        load_x(0, 1)
+        for s in range(1, S):
+            load_x(s, 0)
+            load_x(s, 1)
+        half = G * S // 2
+        for a in (0, half):
+            load_scale_rows(w1s_early[:, a * H : (a + half) * H], w1_rows[a : a + half], H)
+
+        cast(nc.vector.tensor_copy, 0, 0, 256)
+        cast(nc.scalar.copy, 0, 256, CUT)
+        quantise(0, 0, 256)
+        cast(nc.vector.tensor_copy, 0, CUT, WIDE)
+        cast(nc.scalar.copy, 0, WIDE, T)
+        quantise(0, WIDE, T)
+        quantise(0, 256, WIDE)
+
+        def load_w1(tile, e):
+            u = e % G
+            nc.sync.dma_start(
+                out=tile[:, u * S * 2 * H : (u + 1) * S * 2 * H].bitcast(I32).rearrange("p (s n) -> p s n", s=S),
+                in_=w1_words[e].rearrange("s p n -> p s n").bitcast(I32),
+            )
+
+        w1w_early = sbuf([P, G * S * 2 * H], U8, "w1w_early", "raw0a")
+        for s in range(S):
+            nc.sync.dma_start(
+                out=w1w_early[:].bitcast(I32).rearrange("p (u s n) -> p u s n", u=G, s=S)[:, :, s, :],
+                in_=w1_words[0:G, s].rearrange("e p n -> p e n").bitcast(I32),
+            )
+        late_scales = sbuf([P, G * S * H + E * N], U8, "late_scales", "raw0b")
+        nc.gpsimd.memset(late_scales[:].bitcast(I32), 0)
+        load_scale_rows(late_scales[:, 0 : G * S * H], w1_rows[G * S : 2 * G * S], H)
+        w2s = late_scales[:, G * S * H :]
+        load_scale_rows(w2s, w2_scales.rearrange("e s q n -> (e s) q n"), N)
+
+        gather_words(0, 0)
+        gather_scales(0, 0)
+        gather_words(0, 1)
+        round_and_quantise(1)
+        gather_scales(0, 1, "rounded1b")
+        gather_words(1, 0)
+        gather_scales(1, 0)
+        round_and_quantise(2)
+
+        w1w_late = sbuf([P, G * S * 2 * H], U8, "w1w_late", "raw2a")
+        for e in range(G, E):
+            load_w1(w1w_late, e)
+        w2w = sbuf([P, E * 2 * N], U8, "w2w", "raw2b")
+        nc.sync.dma_start(
+            out=w2w[:].bitcast(I32).rearrange("p (e n) -> p e n", e=E), in_=w2_words.rearrange("e s p n -> p (e s) n").bitcast(I32)
+        )
+
+        gather_words(1, 1, "rounded2b")
+        gather_words(2, 0)
+        gather_scales(2, 0)
+        round_and_quantise(3)
+        late_pair = sbuf([P, 2 * G * C], U8, "late_pair", "rounded3b")
+        slot_scales[1, 1] = late_pair[:, 0 : G * C]
+        slot_scales[2, 1] = late_pair[:, G * C :]
+        gather_scales(1, 1)
+        gather_words(3, 0, None, 0, C)
+        gather_scales(3, 0, None, 0, C)
+        gather_words(3, 0, None, C, G * C)
+        gather_scales(3, 0, None, C, G * C)
+        for u in range(G):
+            gather_words(2, 1, "rounded3a", C * u, C * (u + 1))
+            gather_scales(2, 1, None, C * u, C * (u + 1))
+            gather_words(3, 1, None, C * u, C * (u + 1))
+            gather_scales(3, 1, None, C * u, C * (u + 1))
+
+        def first_layer(e, passes=range(S)):
+            g, u = divmod(e, G)
+            w1w = (w1w_early, w1w_late)[g]
+            w1s = (w1s_early, late_scales)[g]
+            for s in passes:
+                a = S * u + s
                 nc.tensor.matmul_mx(
                     out=bank[e][:],
-                    lhsT=slot_words[key][:, C * v : C * (v + 1)].bitcast(E4M3),
-                    lhsT_scale=slot_scales[key][:, C * v : C * (v + 1)],
-                    rhs=w1w[g][:, s, u, :].bitcast(E2M1),
-                    rhs_scale=w1s[g][:, S * u + s, :],
+                    lhsT=slot_words[s, g][:, C * u : C * (u + 1)].bitcast(E4M3),
+                    lhsT_scale=slot_scales[s, g][:, C * u : C * (u + 1)],
+                    rhs=w1w[:, 2 * H * a : 2 * H * (a + 1)].bitcast(E2M1),
+                    rhs_scale=w1s[:, H * a : H * (a + 1)],
                     start=(s == 0),
                     stop=(s == S - 1),
                 )
-
-        def activate(e):
-            nc.scalar.activation(
+            if S - 1 in passes:
+              nc.scalar.activation(
                 hidden[e][:].rearrange("r (u p d) -> r u p d", u=2, d=2), bank[e][:].rearrange("r (p u d) -> r u p d", u=2, d=2), GELU
-            )
+              )
 
         def turn(e):
             pairs = hidden[e][:].bitcast(F32)
             for u in range(2):
                 nc.tensor.transpose(bank[e][:, C * u : C * (u + 1)], pairs[:, P * u : P * (u + 1)], ident[:])
-
-        def unload_turned(e):
-            nc.vector.tensor_copy(
+            nc.scalar.copy(
                 hturned[e][:].rearrange("p c t -> p (c t)").bitcast(F32).rearrange("p (c u) -> p c u", u=2),
                 bank[e][:, 0 : 2 * C].rearrange("p (u c) -> p c u", u=2),
             )
-
-        def requantise(e):
             nc.vector.quantize_mx(out=hwords[e][:].bitcast(E4M3), scales=hscales[e][:], in_=hturned[e][:].rearrange("p c t -> p (c t)"))
 
-        def second_layer(e):
+        def second_layer(e, v, target):
+            nc.tensor.matmul_mx(
+                out=target,
+                lhsT=w2w[:, 2 * N * e + 2 * P * v : 2 * N * e + 2 * P * (v + 1)].bitcast(E2M1),
+                lhsT_scale=w2s[:, N * e + P * v : N * e + P * (v + 1)],
+                rhs=hwords[e][:].bitcast(E4M3),
+                rhs_scale=hscales[e][:],
+                start=True,
+                stop=True,
+            )
+
+        view = out.rearrange("(v p) (m e u) -> v p m e u", v=2, m=R, e=E)
+
+        def store(queue, v, a, b):
+            queue.dma_start(
+                out=view[v][:, :, a:b, :].rearrange("p m e u -> p m (e u)"),
+                in_=result[:, v, :, a:b, :].rearrange("p m e u -> p m (e u)"),
+            )
+
+        for s in range(S - 1):
+            for e in range(G):
+                first_layer(e, (s,))
+        first_layer(0, (S - 1,))
+        for e in range(1, E):
+            first_layer(e, (S - 1,) if e < G else range(S))
+            turn(e - 1)
+        turn(E - 1)
+
+        copies = (nc.vector.tensor_copy, nc.scalar.copy)
+        for v in range(2):
+            for e in range(4):
+                second_layer(e, v, early_out[v][:, C * e : C * (e + 1)])
+            copies[v](result[:, v, :, 0:4, :], early_out[v][:].rearrange("p (e m u) -> p m e u", e=4, m=R))
+            store(nc.sync, v, 0, 4)
+        for e in (4, 5):
             for v in range(2):
-                nc.tensor.matmul_mx(
-                    out=bank[e][:, 2 * C + C * v : 2 * C + C * (v + 1)],
-                    lhsT=w2w[:, e, 2 * P * v : 2 * P * (v + 1)].bitcast(E2M1),
-                    lhsT_scale=w2s[:, e, P * v : P * (v + 1)],
-                    rhs=hwords[e][:].bitcast(E4M3),
-                    rhs_scale=hscales[e][:],
-                    start=True,
-                    stop=True,
-                )
-
-        def unload_result(e):
-            (nc.vector.tensor_copy if e == E - 1 else nc.scalar.copy)(result[:, :, :, e, :], bank[e][:, 2 * C : 4 * C].rearrange("p (v m u) -> p v m u", v=2, m=R))
-
-        def store(a, b):
-            view = out.rearrange("(v p) (m e u) -> v p m e u", v=2, m=R, e=E)
-            for v in range(2):
-                nc.sync.dma_start(
-                    out=view[v][:, :, a:b, :].rearrange("p m e u -> p m (e u)"),
-                    in_=result[:, v, :, a:b, :].rearrange("p m e u -> p m (e u)"),
-                )
-
-        cast(nc.vector.tensor_copy, 0, 0, 384)
-        cast(nc.scalar.copy, 0, 384, 512)
-        cast(nc.scalar.copy, 0, 512, T)
-        quantise(0, 0, 512)
-        quantise(0, 512, T)
-        half = 3 * C
-        gather_tiles((0, 0), 6 * C)
-        gather_words((0, 0), 0, 0, half)
-        gather_words((0, 0), 0, half, 6 * C)
-        gather_scales((0, 0), 0, 0, half)
-        cast(nc.scalar.copy, 1, 0, 512)
-        cast(nc.scalar.copy, 1, 512, T)
-        quantise(1, 0, 512)
-        quantise(1, 512, T)
-        gather_scales((0, 0), 0, half, 6 * C)
-        gather_tiles((1, 0), 6 * C)
-        gather_words((1, 0), 0, 0, half)
-        gather_words((1, 0), 0, half, 6 * C)
-        gather_scales((1, 0), 0, 0, half)
-        cast(nc.scalar.copy, 2, 0, 512)
-        cast(nc.scalar.copy, 2, 512, T)
-        quantise(2, 0, 512)
-        quantise(2, 512, T)
-        gather_scales((1, 0), 0, half, 6 * C)
-        for s in (0, 1):
-            for e in GROUPS[0]:
-                first_layer(e, (s,))
-        gather_tiles((2, 0), 4 * C)
-        gather_words((2, 0), 0, 0, 2 * C)
-        gather_scales((2, 0), 0, 0, 2 * C)
-        gather_words((2, 0), 0, 2 * C, 4 * C)
-        cast(nc.scalar.copy, 3, 0, 512)
-        cast(nc.scalar.copy, 3, 512, T)
-        quantise(3, 0, 512)
-        quantise(3, 512, T)
-        gather_scales((2, 0), 0, 2 * C, 4 * C)
-        gather_tiles((3, 0), 4 * C)
-        for a in (0, 2 * C):
-            gather_words((3, 0), 0, a, a + 2 * C)
-            gather_scales((3, 0), 0, a, a + 2 * C)
-        for s in (2, 3):
-            gather_tiles((s, 1), 2 * C, ring=(s == 2))
-            gather_words((s, 1), 4 * C, 4 * C, 6 * C)
-            gather_scales((s, 1), 4 * C, 4 * C, 6 * C)
-        for s in (2, 3):
-            for e in GROUPS[0]:
-                first_layer(e, (s,))
-        for e in GROUPS[0]:
-            activate(e)
-        for e in GROUPS[0]:
-            turn(e)
-        for s in range(S):
-            for e in GROUPS[1]:
-                first_layer(e, (s,))
-        activate(4)
-        activate(5)
-        for e in GROUPS[0]:
-            unload_turned(e)
-            if e > 0:
-                requantise(e - 1)
-        requantise(3)
-        turn(4)
-        turn(5)
-        unload_turned(4)
-        unload_turned(5)
-        requantise(4)
-        requantise(5)
-        for e in range(4):
-            second_layer(e)
-        for e in range(4):
-            unload_result(e)
-        store(0, 4)
-        second_layer(4)
-        second_layer(5)
-        unload_result(4)
-        unload_result(5)
-        store(4, 6)
+                target = bank[2 * (e - 4) + v]
+                second_layer(e, v, target[:, 0:C])
+                copies[v](result[:, v, :, e, :], target[:, 0:C].rearrange("p (m u) -> p m u", m=R))
+        for v in range(2):
+            store(nc.sync, v, 4, 6)

@@ -18,7 +18,7 @@ K, T, E, C, H, N, R = 2048, 640, 6, 128, 512, 256, 4
 S = K // 512
 U = C // R
 G = 3
-CUT = 384
+CUT = 416
 WIDE = 512
 FLOPS = 2 * E * C * (K * H + H * N)
 
@@ -35,9 +35,10 @@ def tile_moe_eps_mlp_gelu_kernel(tc, xT, w1_words, w1_scales, w2_words, w2_scale
         offsets = keep.tile([P, E * C // 16], U16, name="offsets")
         raw = {}
         rounded = {}
+        pieces = {s: ((0, T),) for s in range(S)}
         for s in range(S):
-            raw[s, 0] = sbuf([P, 4, CUT], F32, f"raw{s}a")
-            raw[s, 1] = sbuf([P, 4, T - CUT], F32, f"raw{s}b")
+            for part, (a, b) in enumerate(pieces[s]):
+                raw[s, part] = sbuf([P, 4, b - a], F32, f"raw{s}{part}")
             rounded[s, 0] = sbuf([P, WIDE, 4], BF16, f"rounded{s}a")
             rounded[s, 1] = sbuf([P, T - WIDE, 4], BF16, f"rounded{s}b")
         words = [sbuf([P, T], U32, f"words{s}") for s in range(S)]
@@ -61,7 +62,7 @@ def tile_moe_eps_mlp_gelu_kernel(tc, xT, w1_words, w1_scales, w2_words, w2_scale
         make_identity(nc, ident[:])
 
         def load_x(s, part):
-            a, b = ((0, CUT), (CUT, T))[part]
+            a, b = pieces[s][part]
             nc.sync.dma_start(out=raw[s, part][:], in_=xT[512 * s : 512 * (s + 1), :].rearrange("(p j) w -> p j w", j=4)[:, :, a:b])
 
         def load_scale_rows(plane, rows, width):
@@ -72,7 +73,7 @@ def tile_moe_eps_mlp_gelu_kernel(tc, xT, w1_words, w1_scales, w2_words, w2_scale
                 )
 
         def raw_view(s, a, b):
-            return raw[s, 0][:, :, a:b] if b <= CUT else raw[s, 1][:, :, a - CUT : b - CUT]
+            return raw[s, 0][:, :, a:b] if b <= pieces[s][0][1] else raw[s, 1][:, :, a - CUT : b - CUT]
 
         def rounded_view(s, a, b):
             return rounded[s, 0][:, a:b, :] if b <= WIDE else rounded[s, 1][:, a - WIDE : b - WIDE, :]
@@ -89,9 +90,9 @@ def tile_moe_eps_mlp_gelu_kernel(tc, xT, w1_words, w1_scales, w2_words, w2_scale
             )
 
         def round_and_quantise(s):
-            cast(nc.scalar.copy, s, 0, CUT)
-            cast(nc.scalar.copy, s, CUT, WIDE)
-            cast(nc.scalar.copy, s, WIDE, T)
+            cuts = sorted({0, pieces[s][0][1], WIDE, T})
+            for a, b in zip(cuts, cuts[1:]):
+                cast(nc.scalar.copy, s, a, b)
             quantise(s, 0, WIDE)
             quantise(s, WIDE, T)
 
@@ -116,57 +117,63 @@ def tile_moe_eps_mlp_gelu_kernel(tc, xT, w1_words, w1_scales, w2_words, w2_scale
 
         load_x(0, 0)
         nc.sync.dma_start(offsets[:], offs)
-        load_x(0, 1)
         for s in range(1, S):
-            load_x(s, 0)
-            load_x(s, 1)
+            for part in range(len(pieces[s])):
+                load_x(s, part)
         half = G * S // 2
         for a in (0, half):
             load_scale_rows(w1s_early[:, a * H : (a + half) * H], w1_rows[a : a + half], H)
 
-        cast(nc.vector.tensor_copy, 0, 0, 256)
-        cast(nc.scalar.copy, 0, 256, CUT)
-        quantise(0, 0, 256)
-        cast(nc.vector.tensor_copy, 0, CUT, WIDE)
+        cast(nc.vector.tensor_copy, 0, 0, CUT)
         cast(nc.scalar.copy, 0, WIDE, T)
+        cast(nc.scalar.copy, 0, CUT, WIDE)
         quantise(0, WIDE, T)
-        quantise(0, 256, WIDE)
+        quantise(0, 0, WIDE)
 
-        def load_w1(tile, e):
+        def load_w1(tile, e, a=0, b=S):
             u = e % G
             nc.sync.dma_start(
-                out=tile[:, u * S * 2 * H : (u + 1) * S * 2 * H].bitcast(I32).rearrange("p (s n) -> p s n", s=S),
-                in_=w1_words[e].rearrange("s p n -> p s n").bitcast(I32),
+                out=tile[:, (u * S + a) * 2 * H : (u * S + b) * 2 * H].bitcast(I32).rearrange("p (s n) -> p s n", s=b - a),
+                in_=w1_words[e, a:b].rearrange("s p n -> p s n").bitcast(I32),
             )
 
-        w1w_early = sbuf([P, G * S * 2 * H], U8, "w1w_early", "raw0a")
-        for s in range(S):
+        def load_w1_pass(tile, g, s):
             nc.sync.dma_start(
-                out=w1w_early[:].bitcast(I32).rearrange("p (u s n) -> p u s n", u=G, s=S)[:, :, s, :],
-                in_=w1_words[0:G, s].rearrange("e p n -> p e n").bitcast(I32),
+                out=tile[:].bitcast(I32).rearrange("p (u s n) -> p u s n", u=G, s=S)[:, :, s, :],
+                in_=w1_words[G * g : G * (g + 1), s].rearrange("e p n -> p e n").bitcast(I32),
             )
-        late_scales = sbuf([P, G * S * H + E * N], U8, "late_scales", "raw0b")
-        nc.gpsimd.memset(late_scales[:].bitcast(I32), 0)
-        load_scale_rows(late_scales[:, 0 : G * S * H], w1_rows[G * S : 2 * G * S], H)
-        w2s = late_scales[:, G * S * H :]
-        load_scale_rows(w2s, w2_scales.rearrange("e s q n -> (e s) q n"), N)
 
+        w1w_early = sbuf([P, G * S * 2 * H], U8, "w1w_early", "raw00")
+        for s in range(S):
+            load_w1_pass(w1w_early, 0, s)
         gather_words(0, 0)
         gather_scales(0, 0)
         gather_words(0, 1)
+        late_scales = sbuf([P, G * S * H], U8, "late_scales", "rounded0b")
+        nc.vector.memset(late_scales[:].bitcast(I32), 0)
+        for a in (0, half):
+            load_scale_rows(late_scales[:, a * H : (a + half) * H], w1_rows[G * S + a : G * S + a + half], H)
         round_and_quantise(1)
         gather_scales(0, 1, "rounded1b")
         gather_words(1, 0)
         gather_scales(1, 0)
         round_and_quantise(2)
 
-        w1w_late = sbuf([P, G * S * 2 * H], U8, "w1w_late", "raw2a")
-        for e in range(G, E):
-            load_w1(w1w_late, e)
-        w2w = sbuf([P, E * 2 * N], U8, "w2w", "raw2b")
+        w1w_late = sbuf([P, G * S * 2 * H], U8, "w1w_late", "raw10")
+        for s in range(2):
+            load_w1_pass(w1w_late, 1, s)
+        for e in range(G, E - 1):
+            load_w1(w1w_late, e, 2, S)
+        load_w1(w1w_late, E - 1, 2, 3)
+        load_w1(w1w_late, E - 1, 3, S)
+        w2w = sbuf([P, E * 2 * N], U8, "w2w", "raw20")
         nc.sync.dma_start(
             out=w2w[:].bitcast(I32).rearrange("p (e n) -> p e n", e=E), in_=w2_words.rearrange("e s p n -> p (e s) n").bitcast(I32)
         )
+
+        w2s = sbuf([P, E * N], U8, "w2s", "rounded2a")
+        nc.vector.memset(w2s[:].bitcast(I32), 0)
+        load_scale_rows(w2s[:], w2_scales.rearrange("e s q n -> (e s) q n"), N)
 
         gather_words(1, 1, "rounded2b")
         gather_words(2, 0)
@@ -210,7 +217,7 @@ def tile_moe_eps_mlp_gelu_kernel(tc, xT, w1_words, w1_scales, w2_words, w2_scale
             pairs = hidden[e][:].bitcast(F32)
             for u in range(2):
                 nc.tensor.transpose(bank[e][:, C * u : C * (u + 1)], pairs[:, P * u : P * (u + 1)], ident[:])
-            nc.scalar.copy(
+            (nc.vector.tensor_copy if G <= e < E - 1 else nc.scalar.copy)(
                 hturned[e][:].rearrange("p c t -> p (c t)").bitcast(F32).rearrange("p (c u) -> p c u", u=2),
                 bank[e][:, 0 : 2 * C].rearrange("p (u c) -> p c u", u=2),
             )
@@ -238,10 +245,15 @@ def tile_moe_eps_mlp_gelu_kernel(tc, xT, w1_words, w1_scales, w2_words, w2_scale
         for s in range(S - 1):
             for e in range(G):
                 first_layer(e, (s,))
-        first_layer(0, (S - 1,))
-        for e in range(1, E):
-            first_layer(e, (S - 1,) if e < G else range(S))
+        for e in range(G):
+            first_layer(e, (S - 1,))
+        for s in range(2):
+            turn(s)
+            for e in range(G, E):
+                first_layer(e, (s,))
+        for e in range(G, E):
             turn(e - 1)
+            first_layer(e, (2, 3))
         turn(E - 1)
 
         copies = (nc.vector.tensor_copy, nc.scalar.copy)
@@ -249,11 +261,10 @@ def tile_moe_eps_mlp_gelu_kernel(tc, xT, w1_words, w1_scales, w2_words, w2_scale
             for e in range(4):
                 second_layer(e, v, early_out[v][:, C * e : C * (e + 1)])
             copies[v](result[:, v, :, 0:4, :], early_out[v][:].rearrange("p (e m u) -> p m e u", e=4, m=R))
-            store(nc.sync, v, 0, 4)
         for e in (4, 5):
             for v in range(2):
                 target = bank[2 * (e - 4) + v]
                 second_layer(e, v, target[:, 0:C])
                 copies[v](result[:, v, :, e, :], target[:, 0:C].rearrange("p (m u) -> p m u", m=R))
         for v in range(2):
-            store(nc.sync, v, 4, 6)
+            store(nc.sync, v, 0, E)

@@ -139,56 +139,55 @@ def tile_moe_eps_mlp_gelu_kernel(tc, xT, w1_words, w1_scales, w2_words, w2_scale
 
         def load_w1_pass(tile, g, s):
             nc.sync.dma_start(
-                out=tile[:].bitcast(I32).rearrange("p (u s n) -> p u s n", u=G, s=S)[:, :, s, :],
+                out=tile.bitcast(I32).rearrange("p (u s n) -> p u s n", u=G, s=S)[:, :, s, :],
                 in_=w1_words[G * g : G * (g + 1), s].rearrange("e p n -> p e n").bitcast(I32),
             )
 
         w1w_early = sbuf([P, G * S * 2 * H], U8, "w1w_early", "raw00")
         for s in range(S):
-            load_w1_pass(w1w_early, 0, s)
-        gather_words(0, 0)
-        gather_scales(0, 0)
-        gather_words(0, 1)
-        late_scales = sbuf([P, G * S * H], U8, "late_scales", "rounded0b")
+            load_w1_pass(w1w_early[:], 0, s)
+        for g in range(2):
+            gather_words(0, g)
+            gather_scales(0, g)
+        round_and_quantise(1)
+        late_scales = sbuf([P, G * S * H], U8, "late_scales", "rounded1b")
         nc.vector.memset(late_scales[:].bitcast(I32), 0)
         for a in (0, half):
             load_scale_rows(late_scales[:, a * H : (a + half) * H], w1_rows[G * S + a : G * S + a + half], H)
-        round_and_quantise(1)
-        gather_scales(0, 1, "rounded1b")
         gather_words(1, 0)
         gather_scales(1, 0)
         round_and_quantise(2)
 
-        w1w_late = sbuf([P, G * S * 2 * H], U8, "w1w_late", "raw10")
+        late_words = sbuf([P, G * S * 2 * H + E * 2 * N], U8, "late_words", "rounded2b")
+        w1w_late = late_words[:, 0 : G * S * 2 * H]
+        w2w = late_words[:, G * S * 2 * H :]
         for s in range(2):
             load_w1_pass(w1w_late, 1, s)
         for e in range(G, E - 1):
             load_w1(w1w_late, e, 2, S)
         load_w1(w1w_late, E - 1, 2, 3)
         load_w1(w1w_late, E - 1, 3, S)
-        w2w = sbuf([P, E * 2 * N], U8, "w2w", "raw20")
-        nc.sync.dma_start(
-            out=w2w[:].bitcast(I32).rearrange("p (e n) -> p e n", e=E), in_=w2_words.rearrange("e s p n -> p (e s) n").bitcast(I32)
-        )
+        nc.sync.dma_start(out=w2w.bitcast(I32).rearrange("p (e n) -> p e n", e=E), in_=w2_words.rearrange("e s p n -> p (e s) n").bitcast(I32))
 
-        w2s = sbuf([P, E * N], U8, "w2s", "rounded2a")
-        nc.vector.memset(w2s[:].bitcast(I32), 0)
-        load_scale_rows(w2s[:], w2_scales.rearrange("e s q n -> (e s) q n"), N)
-
-        gather_words(1, 1, "rounded2b")
         gather_words(2, 0)
         gather_scales(2, 0)
         round_and_quantise(3)
-        late_pair = sbuf([P, 2 * G * C], U8, "late_pair", "rounded3b")
-        slot_scales[1, 1] = late_pair[:, 0 : G * C]
-        slot_scales[2, 1] = late_pair[:, G * C :]
-        gather_scales(1, 1)
+        w2s = sbuf([P, E * N], U8, "w2s", "rounded3b")
+        nc.vector.memset(w2s[:].bitcast(I32), 0)
+        load_scale_rows(w2s[:], w2_scales.rearrange("e s q n -> (e s) q n"), N)
+        word_pair = sbuf([P, 2 * G * C], U32, "word_pair", "rounded3a")
+        scale_pair = sbuf([P, 2 * G * C], U8, "scale_pair", "raw30")
+        for s in (1, 2):
+            slot_words[s, 1] = word_pair[:, (s - 1) * G * C : s * G * C]
+            slot_scales[s, 1] = scale_pair[:, (s - 1) * G * C : s * G * C]
         gather_words(3, 0, None, 0, C)
         gather_scales(3, 0, None, 0, C)
         gather_words(3, 0, None, C, G * C)
         gather_scales(3, 0, None, C, G * C)
+        gather_words(1, 1)
+        gather_scales(1, 1)
         for u in range(G):
-            gather_words(2, 1, "rounded3a", C * u, C * (u + 1))
+            gather_words(2, 1, None, C * u, C * (u + 1))
             gather_scales(2, 1, None, C * u, C * (u + 1))
             gather_words(3, 1, None, C * u, C * (u + 1))
             gather_scales(3, 1, None, C * u, C * (u + 1))

@@ -43,7 +43,6 @@ def tile_moe_eps_mlp_gelu_kernel(tc, xT, w1_words, w1_scales, w2_words, w2_scale
             rounded[s, 1] = sbuf([P, T - WIDE, 4], BF16, f"rounded{s}b")
         words = [sbuf([P, T], U32, f"words{s}") for s in range(S)]
         scales = [sbuf([P, T], U8, f"scales{s}") for s in range(S)]
-        w1s_early = sbuf([P, G * S * H], U8, "w1s_early")
         hidden = [sbuf([P, H], BF16, f"hidden{e}") for e in range(E)]
         hturned = [sbuf([P, C, 4], BF16, f"hturned{e}") for e in range(E)]
         hwords = [sbuf([P, C], U32, f"hwords{e}") for e in range(E)]
@@ -56,7 +55,6 @@ def tile_moe_eps_mlp_gelu_kernel(tc, xT, w1_words, w1_scales, w2_words, w2_scale
 
         nc.vector.memset(warm[:], 0.0)
         nc.scalar.activation(warm[:, 1:2], warm[:, 0:1], GELU)
-        nc.vector.memset(w1s_early[:].bitcast(I32), 0)
         for s in range(S):
             nc.vector.memset(scales[s][:].bitcast(I32), 0)
         make_identity(nc, ident[:])
@@ -120,9 +118,6 @@ def tile_moe_eps_mlp_gelu_kernel(tc, xT, w1_words, w1_scales, w2_words, w2_scale
         for s in range(1, S):
             for part in range(len(pieces[s])):
                 load_x(s, part)
-        half = G * S // 2
-        for a in (0, half):
-            load_scale_rows(w1s_early[:, a * H : (a + half) * H], w1_rows[a : a + half], H)
 
         cast(nc.vector.tensor_copy, 0, 0, CUT)
         cast(nc.scalar.copy, 0, WIDE, T)
@@ -143,22 +138,22 @@ def tile_moe_eps_mlp_gelu_kernel(tc, xT, w1_words, w1_scales, w2_words, w2_scale
                 in_=w1_words[G * g : G * (g + 1), s].rearrange("e p n -> p e n").bitcast(I32),
             )
 
-        w1w_early = sbuf([P, G * S * 2 * H], U8, "w1w_early", "raw00")
+        w1s_early = sbuf([P, G * S * H], U8, "w1s_early", "raw00")
+        load_scale_rows(w1s_early[:], w1_rows[0 : G * S], H)
+        w1w_early = sbuf([P, G * S * 2 * H], U8, "w1w_early", "rounded0a")
         for s in range(S):
             load_w1_pass(w1w_early[:], 0, s)
         for g in range(2):
             gather_words(0, g)
             gather_scales(0, g)
         round_and_quantise(1)
-        late_scales = sbuf([P, G * S * H], U8, "late_scales", "rounded1b")
-        nc.vector.memset(late_scales[:].bitcast(I32), 0)
-        for a in (0, half):
-            load_scale_rows(late_scales[:, a * H : (a + half) * H], w1_rows[G * S + a : G * S + a + half], H)
+        late_scales = sbuf([P, G * S * H], U8, "late_scales", "raw10")
+        load_scale_rows(late_scales[:], w1_rows[G * S : 2 * G * S], H)
         gather_words(1, 0)
         gather_scales(1, 0)
         round_and_quantise(2)
 
-        late_words = sbuf([P, G * S * 2 * H + E * 2 * N], U8, "late_words", "rounded2b")
+        late_words = sbuf([P, G * S * 2 * H + E * 2 * N], U8, "late_words", "raw20")
         w1w_late = late_words[:, 0 : G * S * 2 * H]
         w2w = late_words[:, G * S * 2 * H :]
         for s in range(2):
@@ -172,11 +167,10 @@ def tile_moe_eps_mlp_gelu_kernel(tc, xT, w1_words, w1_scales, w2_words, w2_scale
         gather_words(2, 0)
         gather_scales(2, 0)
         round_and_quantise(3)
-        w2s = sbuf([P, E * N], U8, "w2s", "rounded3b")
-        nc.vector.memset(w2s[:].bitcast(I32), 0)
+        w2s = sbuf([P, E * N], U8, "w2s", "raw30")
         load_scale_rows(w2s[:], w2_scales.rearrange("e s q n -> (e s) q n"), N)
         word_pair = sbuf([P, 2 * G * C], U32, "word_pair", "rounded3a")
-        scale_pair = sbuf([P, 2 * G * C], U8, "scale_pair", "raw30")
+        scale_pair = sbuf([P, 2 * G * C], U8, "scale_pair", "rounded3b")
         for s in (1, 2):
             slot_words[s, 1] = word_pair[:, (s - 1) * G * C : s * G * C]
             slot_scales[s, 1] = scale_pair[:, (s - 1) * G * C : s * G * C]

@@ -49,12 +49,9 @@ def tile_moe_eps_mlp_gelu_kernel(tc, xT, w1_words, w1_scales, w2_words, w2_scale
         hscales = [sbuf([P, C], U8, f"hscales{e}") for e in range(E)]
         result = sbuf([P, 2, R, E, U], F32, "result")
         ident = keep.tile([P, P], F32, name="ident")
-        warm = keep.tile([P, 2], F32, name="warm")
         bank = [psum.tile([P, H], F32, name=f"bank{e}") for e in range(E)]
         early_out = [psum.tile([P, H], F32, name=f"early_out{v}") for v in range(2)]
 
-        nc.vector.memset(warm[:], 0.0)
-        nc.scalar.activation(warm[:, 1:2], warm[:, 0:1], GELU)
         for s in range(S):
             nc.vector.memset(scales[s][:].bitcast(I32), 0)
         make_identity(nc, ident[:])
@@ -115,9 +112,12 @@ def tile_moe_eps_mlp_gelu_kernel(tc, xT, w1_words, w1_scales, w2_words, w2_scale
 
         load_x(0, 0)
         nc.sync.dma_start(offsets[:], offs)
-        for s in range(1, S):
-            for part in range(len(pieces[s])):
-                load_x(s, part)
+        for s in range(1, S - 1):
+            load_x(s, 0)
+        last_rows = xT[512 * (S - 1) :, :].rearrange("(p j) w -> p j w", j=4)
+        nc.sync.dma_start(out=raw[S - 1, 0][:, 0:3, :], in_=last_rows[:, 0:3, :])
+        for a, b in ((0, 256), (256, 512), (512, T)):
+            nc.sync.dma_start(out=raw[S - 1, 0][:, 3, a:b], in_=last_rows[:, 3, a:b])
 
         cast(nc.vector.tensor_copy, 0, 0, CUT)
         cast(nc.scalar.copy, 0, WIDE, T)
@@ -141,8 +141,10 @@ def tile_moe_eps_mlp_gelu_kernel(tc, xT, w1_words, w1_scales, w2_words, w2_scale
         w1s_early = sbuf([P, G * S * H], U8, "w1s_early", "raw00")
         load_scale_rows(w1s_early[:], w1_rows[0 : G * S], H)
         w1w_early = sbuf([P, G * S * 2 * H], U8, "w1w_early", "rounded0a")
-        for s in range(S):
+        for s in range(S - 1):
             load_w1_pass(w1w_early[:], 0, s)
+        for e in range(G):
+            load_w1(w1w_early, e, S - 1, S)
         for g in range(2):
             gather_words(0, g)
             gather_scales(0, g)

@@ -112,12 +112,8 @@ def tile_moe_eps_mlp_gelu_kernel(tc, xT, w1_words, w1_scales, w2_words, w2_scale
 
         load_x(0, 0)
         nc.sync.dma_start(offsets[:], offs)
-        for s in range(1, S - 1):
+        for s in range(1, S):
             load_x(s, 0)
-        last_rows = xT[512 * (S - 1) :, :].rearrange("(p j) w -> p j w", j=4)
-        nc.sync.dma_start(out=raw[S - 1, 0][:, 0:3, :], in_=last_rows[:, 0:3, :])
-        for a, b in ((0, 256), (256, 512), (512, T)):
-            nc.sync.dma_start(out=raw[S - 1, 0][:, 3, a:b], in_=last_rows[:, 3, a:b])
 
         cast(nc.vector.tensor_copy, 0, 0, CUT)
         cast(nc.scalar.copy, 0, WIDE, T)
@@ -132,16 +128,18 @@ def tile_moe_eps_mlp_gelu_kernel(tc, xT, w1_words, w1_scales, w2_words, w2_scale
                 in_=w1_words[e, a:b].rearrange("s p n -> p s n").bitcast(I32),
             )
 
-        def load_w1_pass(tile, g, s):
+        def load_w1_pass(tile, g, s, a=0):
             nc.sync.dma_start(
-                out=tile.bitcast(I32).rearrange("p (u s n) -> p u s n", u=G, s=S)[:, :, s, :],
-                in_=w1_words[G * g : G * (g + 1), s].rearrange("e p n -> p e n").bitcast(I32),
+                out=tile.bitcast(I32).rearrange("p (u s n) -> p u s n", u=G, s=S)[:, a:, s, :],
+                in_=w1_words[G * g + a : G * (g + 1), s].rearrange("e p n -> p e n").bitcast(I32),
             )
 
         w1s_early = sbuf([P, G * S * H], U8, "w1s_early", "raw00")
         load_scale_rows(w1s_early[:], w1_rows[0 : G * S], H)
         w1w_early = sbuf([P, G * S * 2 * H], U8, "w1w_early", "rounded0a")
-        for s in range(S - 1):
+        load_w1(w1w_early, 0, 0, 1)
+        load_w1_pass(w1w_early[:], 0, 0, 1)
+        for s in range(1, S - 1):
             load_w1_pass(w1w_early[:], 0, s)
         for e in range(G):
             load_w1(w1w_early, e, S - 1, S)
@@ -155,22 +153,27 @@ def tile_moe_eps_mlp_gelu_kernel(tc, xT, w1_words, w1_scales, w2_words, w2_scale
         gather_scales(1, 0)
         round_and_quantise(2)
 
-        late_words = sbuf([P, G * S * 2 * H + E * 2 * N], U8, "late_words", "raw20")
-        w1w_late = late_words[:, 0 : G * S * 2 * H]
-        w2w = late_words[:, G * S * 2 * H :]
-        for s in range(2):
-            load_w1_pass(w1w_late, 1, s)
+        late_words = sbuf([P, G * S * 2 * H], U8, "late_words", "raw20")
+        w1w_late = late_words[:]
+        load_w1(w1w_late, G, 0, 1)
+        load_w1_pass(w1w_late, 1, 0, 1)
+        load_w1_pass(w1w_late, 1, 1)
         for e in range(G, E - 1):
             load_w1(w1w_late, e, 2, S)
         load_w1(w1w_late, E - 1, 2, 3)
         load_w1(w1w_late, E - 1, 3, S)
-        nc.sync.dma_start(out=w2w.bitcast(I32).rearrange("p (e n) -> p e n", e=E), in_=w2_words.rearrange("e s p n -> p (e s) n").bitcast(I32))
-
         gather_words(2, 0)
         gather_scales(2, 0)
         round_and_quantise(3)
-        w2s = sbuf([P, E * N], U8, "w2s", "raw30")
-        load_scale_rows(w2s[:], w2_scales.rearrange("e s q n -> (e s) q n"), N)
+        w2_both = sbuf([P, 3 * E * N], U8, "w2_both", "raw30")
+        w2s = w2_both[:, 0 : E * N]
+        w2w = w2_both[:, E * N :]
+        load_scale_rows(w2s, w2_scales.rearrange("e s q n -> (e s) q n"), N)
+        for a, b in ((0, G), (G, E)):
+            nc.sync.dma_start(
+                out=w2w.bitcast(I32).rearrange("p (e n) -> p e n", e=E)[:, a:b, :],
+                in_=w2_words.rearrange("e s p n -> p (e s) n").bitcast(I32)[:, a:b, :],
+            )
         word_pair = sbuf([P, 2 * G * C], U32, "word_pair", "rounded3a")
         scale_pair = sbuf([P, 2 * G * C], U8, "scale_pair", "rounded3b")
         for s in (1, 2):
@@ -182,9 +185,9 @@ def tile_moe_eps_mlp_gelu_kernel(tc, xT, w1_words, w1_scales, w2_words, w2_scale
         gather_scales(3, 0, None, C, G * C)
         gather_words(1, 1)
         gather_scales(1, 1)
+        gather_words(2, 1)
+        gather_scales(2, 1)
         for u in range(G):
-            gather_words(2, 1, None, C * u, C * (u + 1))
-            gather_scales(2, 1, None, C * u, C * (u + 1))
             gather_words(3, 1, None, C * u, C * (u + 1))
             gather_scales(3, 1, None, C * u, C * (u + 1))
 
@@ -208,11 +211,11 @@ def tile_moe_eps_mlp_gelu_kernel(tc, xT, w1_words, w1_scales, w2_words, w2_scale
                 hidden[e][:].rearrange("r (u p d) -> r u p d", u=2, d=2), bank[e][:].rearrange("r (p u d) -> r u p d", u=2, d=2), GELU
               )
 
-        def turn(e):
+        def turn(e, identity):
             pairs = hidden[e][:].bitcast(F32)
             for u in range(2):
-                nc.tensor.transpose(bank[e][:, C * u : C * (u + 1)], pairs[:, P * u : P * (u + 1)], ident[:])
-            (nc.vector.tensor_copy if G <= e < E - 1 else nc.scalar.copy)(
+                nc.tensor.transpose(bank[e][:, C * u : C * (u + 1)], pairs[:, P * u : P * (u + 1)], identity[:])
+            (nc.vector.tensor_copy if e == G else nc.scalar.copy)(
                 hturned[e][:].rearrange("p c t -> p (c t)").bitcast(F32).rearrange("p (c u) -> p c u", u=2),
                 bank[e][:, 0 : 2 * C].rearrange("p (u c) -> p c u", u=2),
             )
@@ -243,23 +246,26 @@ def tile_moe_eps_mlp_gelu_kernel(tc, xT, w1_words, w1_scales, w2_words, w2_scale
         for e in range(G):
             first_layer(e, (S - 1,))
         for s in range(2):
-            turn(s)
             for e in range(G, E):
                 first_layer(e, (s,))
         for e in range(G, E):
-            turn(e - 1)
             first_layer(e, (2, 3))
-        turn(E - 1)
+        ident_mid = sbuf([P, P], F32, "ident_mid", "slot_words01")
+        ident_end = sbuf([P, P], F32, "ident_end", "slot_words31")
+        turn(0, ident)
+        turn(1, ident)
+        nc.scalar.copy(ident_mid[:], ident[:])
+        turn(2, ident_mid)
+        nc.vector.tensor_copy(ident_end[:], ident[:])
+        turn(3, ident_end)
+        turn(4, ident_end)
+        turn(5, ident)
 
         copies = (nc.vector.tensor_copy, nc.scalar.copy)
-        for v in range(2):
-            for e in range(4):
-                second_layer(e, v, early_out[v][:, C * e : C * (e + 1)])
-            copies[v](result[:, v, :, 0:4, :], early_out[v][:].rearrange("p (e m u) -> p m e u", e=4, m=R))
-        for e in (4, 5):
+        for a, b, targets in ((0, 3, early_out), (3, 5, bank[0:2]), (5, 6, bank[2:4])):
             for v in range(2):
-                target = bank[2 * (e - 4) + v]
-                second_layer(e, v, target[:, 0:C])
-                copies[v](result[:, v, :, e, :], target[:, 0:C].rearrange("p (m u) -> p m u", m=R))
+                for e in range(a, b):
+                    second_layer(e, v, targets[v][:, C * (e - a) : C * (e - a + 1)])
+                copies[v](result[:, v, :, a:b, :], targets[v][:, 0 : C * (b - a)].rearrange("p (e m u) -> p m e u", e=b - a, m=R))
         for v in range(2):
             store(nc.sync, v, 0, E)

@@ -30,7 +30,7 @@ def tile_moe_eps_mlp_gelu_kernel(tc, xT, w1_words, w1_scales, w2_words, w2_scale
         psum = ctx.enter_context(tc.psum_pool(name="psum", bufs=1))
 
         def sbuf(shape, dtype, name, tag=None):
-            return keep.tile(shape, dtype, name=name, tag=tag or name, align_bytes=64)
+            return keep.tile(shape, dtype, name=name, tag=tag or name, align_bytes=256)
 
         offsets = keep.tile([P, E * C // 16], U16, name="offsets")
         raw = {}
@@ -112,8 +112,12 @@ def tile_moe_eps_mlp_gelu_kernel(tc, xT, w1_words, w1_scales, w2_words, w2_scale
 
         load_x(0, 0)
         nc.sync.dma_start(offsets[:], offs)
-        for s in range(1, S):
+        for s in range(1, S - 1):
             load_x(s, 0)
+        last_rows = xT[512 * (S - 1) :, :].rearrange("(p j) w -> p j w", j=4)
+        nc.sync.dma_start(out=raw[S - 1, 0][:, 0:3, :], in_=last_rows[:, 0:3, :])
+        for a, b in ((0, 256), (256, 512), (512, T)):
+            nc.sync.dma_start(out=raw[S - 1, 0][:, 3, a:b], in_=last_rows[:, 3, a:b])
 
         cast(nc.vector.tensor_copy, 0, 0, CUT)
         cast(nc.scalar.copy, 0, WIDE, T)

@@ -18,7 +18,8 @@ K, T, E, C, H, N, R = 2048, 640, 6, 128, 512, 256, 4
 S = K // 512
 U = C // R
 G = 3
-CUT = 416
+LAST = S - 1
+SHARE = 416
 WIDE = 512
 FLOPS = 2 * E * C * (K * H + H * N)
 
@@ -33,12 +34,10 @@ def tile_moe_eps_mlp_gelu_kernel(tc, xT, w1_words, w1_scales, w2_words, w2_scale
             return keep.tile(shape, dtype, name=name, tag=tag or name, align_bytes=256)
 
         offsets = keep.tile([P, E * C // 16], U16, name="offsets")
-        raw = {}
+        raw = []
         rounded = {}
-        pieces = {s: ((0, T),) for s in range(S)}
         for s in range(S):
-            for part, (a, b) in enumerate(pieces[s]):
-                raw[s, part] = sbuf([P, 4, b - a], F32, f"raw{s}{part}")
+            raw.append(sbuf([P, 4, T], F32, f"raw{s}0"))
             rounded[s, 0] = sbuf([P, WIDE, 4], BF16, f"rounded{s}a")
             rounded[s, 1] = sbuf([P, T - WIDE, 4], BF16, f"rounded{s}b")
         words = [sbuf([P, T], U32, f"words{s}") for s in range(S)]
@@ -56,9 +55,8 @@ def tile_moe_eps_mlp_gelu_kernel(tc, xT, w1_words, w1_scales, w2_words, w2_scale
             nc.vector.memset(scales[s][:].bitcast(I32), 0)
         make_identity(nc, ident[:])
 
-        def load_x(s, part):
-            a, b = pieces[s][part]
-            nc.sync.dma_start(out=raw[s, part][:], in_=xT[512 * s : 512 * (s + 1), :].rearrange("(p j) w -> p j w", j=4)[:, :, a:b])
+        def x_rows(s):
+            return xT[512 * s : 512 * (s + 1), :].rearrange("(p j) w -> p j w", j=4)
 
         def load_scale_rows(plane, rows, width):
             for r in range(4):
@@ -67,16 +65,13 @@ def tile_moe_eps_mlp_gelu_kernel(tc, xT, w1_words, w1_scales, w2_words, w2_scale
                     in_=rows[:, r:16:4, :].rearrange("a q i -> q a i").bitcast(I32),
                 )
 
-        def raw_view(s, a, b):
-            return raw[s, 0][:, :, a:b] if b <= pieces[s][0][1] else raw[s, 1][:, :, a - CUT : b - CUT]
-
         def rounded_view(s, a, b):
             return rounded[s, 0][:, a:b, :] if b <= WIDE else rounded[s, 1][:, a - WIDE : b - WIDE, :]
 
         def cast(engine_copy, s, a, b):
             engine_copy(
                 rounded_view(s, a, b).rearrange("p (c i) t -> p c t i", i=4),
-                raw_view(s, a, b).rearrange("p t (c i) -> p c t i", i=4),
+                raw[s][:, :, a:b].rearrange("p t (c i) -> p c t i", i=4),
             )
 
         def quantise(s, a, b):
@@ -85,120 +80,113 @@ def tile_moe_eps_mlp_gelu_kernel(tc, xT, w1_words, w1_scales, w2_words, w2_scale
             )
 
         def round_and_quantise(s):
-            cuts = sorted({0, pieces[s][0][1], WIDE, T})
-            for a, b in zip(cuts, cuts[1:]):
-                cast(nc.scalar.copy, s, a, b)
+            cast(nc.scalar.copy, s, 0, WIDE)
+            cast(nc.scalar.copy, s, WIDE, T)
             quantise(s, 0, WIDE)
             quantise(s, WIDE, T)
 
         slot_words = {}
         slot_scales = {}
 
-        def gather(dst, table, g, a=0, b=G * C):
-            first = G * C * g
-            nc.vector.tensor_copy(dst[:, a:b], table[:].indirect(offsets[:, (first + a) // 16 : (first + b) // 16]))
-
-        def gather_words(s, g, tag=None, a=0, b=G * C):
+        def gather(s, g, a=0, b=G * C):
+            picks = offsets[:, (G * C * g + a) // 16 : (G * C * g + b) // 16]
             if (s, g) not in slot_words:
-                slot_words[s, g] = sbuf([P, G * C], U32, f"slot_words{s}{g}", tag)[:]
-            gather(slot_words[s, g], words[s], g, a, b)
-
-        def gather_scales(s, g, tag=None, a=0, b=G * C):
+                slot_words[s, g] = sbuf([P, G * C], U32, f"slot_words{s}{g}")[:]
+            nc.vector.tensor_copy(slot_words[s, g][:, a:b], words[s][:].indirect(picks))
             if (s, g) not in slot_scales:
-                slot_scales[s, g] = sbuf([P, G * C], U8, f"slot_scales{s}{g}", tag)[:]
-            gather(slot_scales[s, g], scales[s], g, a, b)
+                slot_scales[s, g] = sbuf([P, G * C], U8, f"slot_scales{s}{g}")[:]
+            nc.vector.tensor_copy(slot_scales[s, g][:, a:b], scales[s][:].indirect(picks))
 
-        w1_rows = w1_scales.rearrange("e s q i -> (e s) q i")
-
-        load_x(0, 0)
-        nc.sync.dma_start(offsets[:], offs)
-        for s in range(1, S - 1):
-            load_x(s, 0)
-        last_rows = xT[512 * (S - 1) :, :].rearrange("(p j) w -> p j w", j=4)
-        nc.sync.dma_start(out=raw[S - 1, 0][:, 0:3, :], in_=last_rows[:, 0:3, :])
-        for a, b in ((0, 256), (256, 512), (512, T)):
-            nc.sync.dma_start(out=raw[S - 1, 0][:, 3, a:b], in_=last_rows[:, 3, a:b])
-
-        cast(nc.vector.tensor_copy, 0, 0, CUT)
-        cast(nc.scalar.copy, 0, WIDE, T)
-        cast(nc.scalar.copy, 0, CUT, WIDE)
-        quantise(0, WIDE, T)
-        quantise(0, 0, WIDE)
-
-        def load_w1(tile, e, a=0, b=S):
+        def load_w1_expert(tile, e, a, b):
             u = e % G
             nc.sync.dma_start(
                 out=tile[:, (u * S + a) * 2 * H : (u * S + b) * 2 * H].bitcast(I32).rearrange("p (s n) -> p s n", s=b - a),
                 in_=w1_words[e, a:b].rearrange("s p n -> p s n").bitcast(I32),
             )
 
-        def load_w1_pass(tile, g, s, a=0):
+        def load_w1_pass(tile, g, s, first=0):
             nc.sync.dma_start(
-                out=tile.bitcast(I32).rearrange("p (u s n) -> p u s n", u=G, s=S)[:, a:, s, :],
-                in_=w1_words[G * g + a : G * (g + 1), s].rearrange("e p n -> p e n").bitcast(I32),
+                out=tile.bitcast(I32).rearrange("p (u s n) -> p u s n", u=G, s=S)[:, first:, s, :],
+                in_=w1_words[G * g + first : G * (g + 1), s].rearrange("e p n -> p e n").bitcast(I32),
             )
+
+        w1_rows = w1_scales.rearrange("e s q i -> (e s) q i")
+
+        nc.sync.dma_start(out=raw[0][:], in_=x_rows(0))
+        nc.sync.dma_start(offsets[:], offs)
+        for s in range(1, LAST):
+            nc.sync.dma_start(out=raw[s][:], in_=x_rows(s))
+        nc.sync.dma_start(out=raw[LAST][:, 0:3, :], in_=x_rows(LAST)[:, 0:3, :])
+        for a, b in ((0, 256), (256, WIDE), (WIDE, T)):
+            nc.sync.dma_start(out=raw[LAST][:, 3, a:b], in_=x_rows(LAST)[:, 3, a:b])
+
+        cast(nc.vector.tensor_copy, 0, 0, SHARE)
+        cast(nc.scalar.copy, 0, WIDE, T)
+        cast(nc.scalar.copy, 0, SHARE, WIDE)
+        quantise(0, WIDE, T)
+        quantise(0, 0, WIDE)
 
         w1s_early = sbuf([P, G * S * H], U8, "w1s_early", "raw00")
         load_scale_rows(w1s_early[:], w1_rows[0 : G * S], H)
         w1w_early = sbuf([P, G * S * 2 * H], U8, "w1w_early", "rounded0a")
-        load_w1(w1w_early, 0, 0, 1)
+        load_w1_expert(w1w_early, 0, 0, 1)
         load_w1_pass(w1w_early[:], 0, 0, 1)
-        for s in range(1, S - 1):
+        for s in range(1, LAST):
             load_w1_pass(w1w_early[:], 0, s)
-        for e in range(G):
-            load_w1(w1w_early, e, S - 1, S)
+        for e in range(G - 1):
+            load_w1_expert(w1w_early, e, LAST, S)
+        for a in (0, H):
+            first = (G * S - 1) * 2 * H + a
+            nc.sync.dma_start(out=w1w_early[:, first : first + H].bitcast(I32), in_=w1_words[G - 1, LAST][:, a : a + H].bitcast(I32))
         for g in range(2):
-            gather_words(0, g)
-            gather_scales(0, g)
+            gather(0, g)
         round_and_quantise(1)
-        late_scales = sbuf([P, G * S * H], U8, "late_scales", "raw10")
-        load_scale_rows(late_scales[:], w1_rows[G * S : 2 * G * S], H)
-        gather_words(1, 0)
-        gather_scales(1, 0)
+        w1s_late = sbuf([P, G * S * H], U8, "late_scales", "raw10")
+        load_scale_rows(w1s_late[:], w1_rows[G * S : 2 * G * S], H)
+        gather(1, 0)
         round_and_quantise(2)
 
-        late_words = sbuf([P, G * S * 2 * H], U8, "late_words", "raw20")
-        w1w_late = late_words[:]
-        load_w1(w1w_late, G, 0, 1)
+        w1w_late = sbuf([P, G * S * 2 * H], U8, "late_words", "raw20")[:]
+        load_w1_expert(w1w_late, G, 0, 1)
         load_w1_pass(w1w_late, 1, 0, 1)
         load_w1_pass(w1w_late, 1, 1)
         for e in range(G, E - 1):
-            load_w1(w1w_late, e, 2, S)
-        load_w1(w1w_late, E - 1, 2, 3)
-        load_w1(w1w_late, E - 1, 3, S)
-        gather_words(2, 0)
-        gather_scales(2, 0)
-        round_and_quantise(3)
+            load_w1_expert(w1w_late, e, 2, S)
+        load_w1_expert(w1w_late, E - 1, 2, LAST)
+        load_w1_expert(w1w_late, E - 1, LAST, S)
+        gather(2, 0)
+        round_and_quantise(LAST)
+
         w2_both = sbuf([P, 3 * E * N], U8, "w2_both", "raw30")
         w2s = w2_both[:, 0 : E * N]
         w2w = w2_both[:, E * N :]
-        load_scale_rows(w2s, w2_scales.rearrange("e s q n -> (e s) q n"), N)
-        for a, b in ((0, G), (G, E)):
+
+        def load_w2(a, b):
             nc.sync.dma_start(
                 out=w2w.bitcast(I32).rearrange("p (e n) -> p e n", e=E)[:, a:b, :],
                 in_=w2_words.rearrange("e s p n -> p (e s) n").bitcast(I32)[:, a:b, :],
             )
+
+        load_w2(0, E - 1)
+        load_scale_rows(w2s, w2_scales.rearrange("e s q n -> (e s) q n"), N)
+        load_w2(E - 1, E)
+
         word_pair = sbuf([P, 2 * G * C], U32, "word_pair", "rounded3a")
         scale_pair = sbuf([P, 2 * G * C], U8, "scale_pair", "rounded3b")
         for s in (1, 2):
             slot_words[s, 1] = word_pair[:, (s - 1) * G * C : s * G * C]
             slot_scales[s, 1] = scale_pair[:, (s - 1) * G * C : s * G * C]
-        gather_words(3, 0, None, 0, C)
-        gather_scales(3, 0, None, 0, C)
-        gather_words(3, 0, None, C, G * C)
-        gather_scales(3, 0, None, C, G * C)
-        gather_words(1, 1)
-        gather_scales(1, 1)
-        gather_words(2, 1)
-        gather_scales(2, 1)
+        gather(LAST, 0, 0, C)
+        gather(LAST, 0, C, G * C)
+        gather(1, 1)
+        gather(2, 1)
         for u in range(G):
-            gather_words(3, 1, None, C * u, C * (u + 1))
-            gather_scales(3, 1, None, C * u, C * (u + 1))
+            gather(LAST, 1, C * u, C * (u + 1))
 
-        def first_layer(e, passes=range(S)):
+        def first_layer(e, passes):
             g, u = divmod(e, G)
             w1w = (w1w_early, w1w_late)[g]
-            w1s = (w1s_early, late_scales)[g]
+            w1s = (w1s_early, w1s_late)[g]
             for s in passes:
                 a = S * u + s
                 nc.tensor.matmul_mx(
@@ -208,20 +196,22 @@ def tile_moe_eps_mlp_gelu_kernel(tc, xT, w1_words, w1_scales, w2_words, w2_scale
                     rhs=w1w[:, 2 * H * a : 2 * H * (a + 1)].bitcast(E2M1),
                     rhs_scale=w1s[:, H * a : H * (a + 1)],
                     start=(s == 0),
-                    stop=(s == S - 1),
+                    stop=(s == LAST),
                 )
-            if S - 1 in passes:
-              nc.scalar.activation(
-                hidden[e][:].rearrange("r (u p d) -> r u p d", u=2, d=2), bank[e][:].rearrange("r (p u d) -> r u p d", u=2, d=2), GELU
-              )
+            if LAST in passes:
+                nc.scalar.activation(
+                    hidden[e][:].rearrange("r (half p d) -> r half p d", half=2, d=2),
+                    bank[e][:].rearrange("r (p half d) -> r half p d", half=2, d=2),
+                    GELU,
+                )
 
-        def turn(e, identity):
+        def turn(e, identity, engine_copy):
             pairs = hidden[e][:].bitcast(F32)
-            for u in range(2):
-                nc.tensor.transpose(bank[e][:, C * u : C * (u + 1)], pairs[:, P * u : P * (u + 1)], identity[:])
-            (nc.vector.tensor_copy if e == G else nc.scalar.copy)(
-                hturned[e][:].rearrange("p c t -> p (c t)").bitcast(F32).rearrange("p (c u) -> p c u", u=2),
-                bank[e][:, 0 : 2 * C].rearrange("p (u c) -> p c u", u=2),
+            for half in range(2):
+                nc.tensor.transpose(bank[e][:, C * half : C * (half + 1)], pairs[:, P * half : P * (half + 1)], identity[:])
+            engine_copy(
+                hturned[e][:].rearrange("p c t -> p (c t)").bitcast(F32).rearrange("p (c half) -> p c half", half=2),
+                bank[e][:, 0 : 2 * C].rearrange("p (half c) -> p c half", half=2),
             )
             nc.vector.quantize_mx(out=hwords[e][:].bitcast(E4M3), scales=hscales[e][:], in_=hturned[e][:].rearrange("p c t -> p (c t)"))
 
@@ -236,40 +226,36 @@ def tile_moe_eps_mlp_gelu_kernel(tc, xT, w1_words, w1_scales, w2_words, w2_scale
                 stop=True,
             )
 
-        view = out.rearrange("(v p) (m e u) -> v p m e u", v=2, m=R, e=E)
-
-        def store(queue, v, a, b):
-            queue.dma_start(
-                out=view[v][:, :, a:b, :].rearrange("p m e u -> p m (e u)"),
-                in_=result[:, v, :, a:b, :].rearrange("p m e u -> p m (e u)"),
-            )
-
-        for s in range(S - 1):
+        for s in range(S):
             for e in range(G):
                 first_layer(e, (s,))
-        for e in range(G):
-            first_layer(e, (S - 1,))
         for s in range(2):
             for e in range(G, E):
                 first_layer(e, (s,))
         for e in range(G, E):
-            first_layer(e, (2, 3))
+            first_layer(e, (2, LAST))
+
         ident_mid = sbuf([P, P], F32, "ident_mid", "slot_words01")
         ident_end = sbuf([P, P], F32, "ident_end", "slot_words31")
-        turn(0, ident)
-        turn(1, ident)
+        turn(0, ident, nc.scalar.copy)
+        turn(1, ident, nc.scalar.copy)
         nc.scalar.copy(ident_mid[:], ident[:])
-        turn(2, ident_mid)
+        turn(2, ident_mid, nc.scalar.copy)
         nc.vector.tensor_copy(ident_end[:], ident[:])
-        turn(3, ident_end)
-        turn(4, ident_end)
-        turn(5, ident)
+        turn(3, ident_end, nc.vector.tensor_copy)
+        turn(4, ident_end, nc.scalar.copy)
+        turn(5, ident, nc.scalar.copy)
 
         copies = (nc.vector.tensor_copy, nc.scalar.copy)
-        for a, b, targets in ((0, 3, early_out), (3, 5, bank[0:2]), (5, 6, bank[2:4])):
+        for a, b, targets in ((0, G, early_out), (G, E - 1, bank[0:2]), (E - 1, E, bank[2:4])):
             for v in range(2):
                 for e in range(a, b):
                     second_layer(e, v, targets[v][:, C * (e - a) : C * (e - a + 1)])
                 copies[v](result[:, v, :, a:b, :], targets[v][:, 0 : C * (b - a)].rearrange("p (e m u) -> p m e u", e=b - a, m=R))
+
+        rows_out = out.rearrange("(v p) (m e u) -> v p m e u", v=2, m=R, e=E)
         for v in range(2):
-            store(nc.sync, v, 0, E)
+            nc.sync.dma_start(
+                out=rows_out[v].rearrange("p m e u -> p m (e u)"),
+                in_=result[:, v, :, :, :].rearrange("p m e u -> p m (e u)"),
+            )

@@ -17,10 +17,12 @@ P = 128
 K, T, E, C, H, N, R = 2048, 640, 6, 128, 512, 256, 4
 S = K // 512
 U = C // R
-G = 3
+EARLY = 4
 LAST = S - 1
 SHARE = 416
 WIDE = 512
+PIECE = 2 * H
+WINDOW = (1024, 704, 704, 704)
 FLOPS = 2 * E * C * (K * H + H * N)
 
 
@@ -28,35 +30,32 @@ def tile_moe_eps_mlp_gelu_kernel(tc, xT, w1_words, w1_scales, w2_words, w2_scale
     nc = tc.nc
     with ExitStack() as ctx:
         keep = ctx.enter_context(tc.tile_pool(name="keep", bufs=1))
+        placed = ctx.enter_context(tc.tile_pool(name="placed", bufs=1))
         psum = ctx.enter_context(tc.psum_pool(name="psum", bufs=1))
 
         def sbuf(shape, dtype, name, tag=None):
             return keep.tile(shape, dtype, name=name, tag=tag or name, align_bytes=256)
 
         offsets = keep.tile([P, E * C // 16], U16, name="offsets")
-        raw = []
+        raw = [placed.tile([P, 4, T], F32, name="raw0", offset=0, align_bytes=256)] + [sbuf([P, 4, T], F32, f"raw{s}") for s in range(1, S)]
         rounded = {}
         for s in range(S):
-            raw.append(sbuf([P, 4, T], F32, f"raw{s}0"))
             rounded[s, 0] = sbuf([P, WIDE, 4], BF16, f"rounded{s}a")
             rounded[s, 1] = sbuf([P, T - WIDE, 4], BF16, f"rounded{s}b")
-        words = [sbuf([P, T], U32, f"words{s}") for s in range(S)]
-        scales = [sbuf([P, T], U8, f"scales{s}") for s in range(S)]
+        words = [sbuf([P, WINDOW[s]], U32, f"words{s}") for s in range(S)]
+        scales = [sbuf([P, WINDOW[s]], U8, f"scales{s}") for s in range(S)]
         hidden = [sbuf([P, H], BF16, f"hidden{e}") for e in range(E)]
-        hturned = [sbuf([P, C, 4], BF16, f"hturned{e}") for e in range(E)]
-        hwords = [sbuf([P, C], U32, f"hwords{e}") for e in range(E)]
-        hscales = [sbuf([P, C], U8, f"hscales{e}") for e in range(E)]
-        result = sbuf([P, 2, R, E, U], F32, "result")
         ident = keep.tile([P, P], F32, name="ident")
-        bank = [psum.tile([P, H], F32, name=f"bank{e}") for e in range(E)]
-        early_out = [psum.tile([P, H], F32, name=f"early_out{v}") for v in range(2)]
+        result = sbuf([P, 2, R, E, U], F32, "result")
+        bank = [psum.tile([P, H], F32, name=f"bank{b}") for b in range(8)]
 
         for s in range(S):
             nc.vector.memset(scales[s][:].bitcast(I32), 0)
+            nc.vector.memset(words[s][:, T:].bitcast(I32), 0)
         make_identity(nc, ident[:])
 
-        def x_rows(s):
-            return xT[512 * s : 512 * (s + 1), :].rearrange("(p j) w -> p j w", j=4)
+        def load_x(s):
+            nc.sync.dma_start(out=raw[s][:], in_=xT[512 * s : 512 * (s + 1), :].rearrange("(p j) w -> p j w", j=4))
 
         def load_scale_rows(plane, rows, width):
             for r in range(4):
@@ -64,6 +63,26 @@ def tile_moe_eps_mlp_gelu_kernel(tc, xT, w1_words, w1_scales, w2_words, w2_scale
                     out=plane[r:P:32].bitcast(I32).rearrange("q (a i) -> q a i", i=width // 4),
                     in_=rows[:, r:16:4, :].rearrange("a q i -> q a i").bitcast(I32),
                 )
+
+        w1_pieces = w1_words.rearrange("e s p n -> p (e s) n").bitcast(I32)
+        w1_rows = w1_scales.rearrange("e s q i -> (e s) q i")
+        piece = {}
+
+        def load_w1(tile, place, pieces):
+            at = [S * e + s for e, s in pieces]
+            step = at[1] - at[0] if len(at) > 1 else 1
+            nc.sync.dma_start(
+                out=tile[:, place * PIECE : (place + len(at)) * PIECE].bitcast(I32).rearrange("p (a n) -> p a n", a=len(at)),
+                in_=w1_pieces[:, at[0] : at[-1] + 1 : step, :],
+            )
+            for j, key in enumerate(pieces):
+                piece[key] = tile[:, (place + j) * PIECE : (place + j + 1) * PIECE]
+            return place + len(at)
+
+        def load_w1_all(tile, loads):
+            place = 0
+            for pieces in loads:
+                place = load_w1(tile, place, pieces)
 
         def rounded_view(s, a, b):
             return rounded[s, 0][:, a:b, :] if b <= WIDE else rounded[s, 1][:, a - WIDE : b - WIDE, :]
@@ -88,37 +107,24 @@ def tile_moe_eps_mlp_gelu_kernel(tc, xT, w1_words, w1_scales, w2_words, w2_scale
         slot_words = {}
         slot_scales = {}
 
-        def gather(s, g, a=0, b=G * C):
-            picks = offsets[:, (G * C * g + a) // 16 : (G * C * g + b) // 16]
-            if (s, g) not in slot_words:
-                slot_words[s, g] = sbuf([P, G * C], U32, f"slot_words{s}{g}")[:]
-            nc.vector.tensor_copy(slot_words[s, g][:, a:b], words[s][:].indirect(picks))
-            if (s, g) not in slot_scales:
-                slot_scales[s, g] = sbuf([P, G * C], U8, f"slot_scales{s}{g}")[:]
-            nc.vector.tensor_copy(slot_scales[s, g][:, a:b], scales[s][:].indirect(picks))
+        def gather(s, first, last, word_tile=None, scale_tile=None):
+            width = C * (last - first)
+            picks = offsets[:, C * first // 16 : C * last // 16]
+            if word_tile is None:
+                word_tile = sbuf([P, width], U32, f"slot_words{s}{first}")[:]
+                scale_tile = sbuf([P, width], U8, f"slot_scales{s}{first}")[:]
+            nc.vector.tensor_copy(word_tile, words[s][:].indirect(picks))
+            nc.vector.tensor_copy(scale_tile, scales[s][:].indirect(picks))
+            for e in range(first, last):
+                slot_words[s, e] = word_tile[:, C * (e - first) : C * (e - first + 1)]
+                slot_scales[s, e] = scale_tile[:, C * (e - first) : C * (e - first + 1)]
 
-        def load_w1_expert(tile, e, a, b):
-            u = e % G
-            nc.sync.dma_start(
-                out=tile[:, (u * S + a) * 2 * H : (u * S + b) * 2 * H].bitcast(I32).rearrange("p (s n) -> p s n", s=b - a),
-                in_=w1_words[e, a:b].rearrange("s p n -> p s n").bitcast(I32),
-            )
-
-        def load_w1_pass(tile, g, s, first=0):
-            nc.sync.dma_start(
-                out=tile.bitcast(I32).rearrange("p (u s n) -> p u s n", u=G, s=S)[:, first:, s, :],
-                in_=w1_words[G * g + first : G * (g + 1), s].rearrange("e p n -> p e n").bitcast(I32),
-            )
-
-        w1_rows = w1_scales.rearrange("e s q i -> (e s) q i")
-
-        nc.sync.dma_start(out=raw[0][:], in_=x_rows(0))
+        load_x(0)
         nc.sync.dma_start(offsets[:], offs)
-        for s in range(1, LAST):
-            nc.sync.dma_start(out=raw[s][:], in_=x_rows(s))
-        nc.sync.dma_start(out=raw[LAST][:, 0:3, :], in_=x_rows(LAST)[:, 0:3, :])
-        for a, b in ((0, 256), (256, WIDE), (WIDE, T)):
-            nc.sync.dma_start(out=raw[LAST][:, 3, a:b], in_=x_rows(LAST)[:, 3, a:b])
+        for s in range(1, S):
+            load_x(s)
+        w1_ahead = sbuf([P, 4 * PIECE], U8, "w1_ahead")
+        load_w1_all(w1_ahead, [[(0, s), (1, s)] for s in range(2)])
 
         cast(nc.vector.tensor_copy, 0, 0, SHARE)
         cast(nc.scalar.copy, 0, WIDE, T)
@@ -126,136 +132,131 @@ def tile_moe_eps_mlp_gelu_kernel(tc, xT, w1_words, w1_scales, w2_words, w2_scale
         quantise(0, WIDE, T)
         quantise(0, 0, WIDE)
 
-        w1s_early = sbuf([P, G * S * H], U8, "w1s_early", "raw00")
-        load_scale_rows(w1s_early[:], w1_rows[0 : G * S], H)
-        w1w_early = sbuf([P, G * S * 2 * H], U8, "w1w_early", "rounded0a")
-        load_w1_expert(w1w_early, 0, 0, 1)
-        load_w1_pass(w1w_early[:], 0, 0, 1)
-        for s in range(1, LAST):
-            load_w1_pass(w1w_early[:], 0, s)
-        for e in range(G - 1):
-            load_w1_expert(w1w_early, e, LAST, S)
-        for a in (0, H):
-            first = (G * S - 1) * 2 * H + a
-            nc.sync.dma_start(out=w1w_early[:, first : first + H].bitcast(I32), in_=w1_words[G - 1, LAST][:, a : a + H].bitcast(I32))
-        for g in range(2):
-            gather(0, g)
+        w1s = []
+        for pair in range(2):
+            w1s.append(placed.tile([P, 2 * S * H], U8, name=f"w1s{pair}", offset=2 * S * H * pair, align_bytes=256))
+            load_scale_rows(w1s[pair][:], w1_rows[2 * S * pair : 2 * S * (pair + 1)], H)
+        w1_early = sbuf([P, 12 * PIECE], U8, "w1_early", "rounded0a")
+        load_w1_all(
+            w1_early,
+            [[(2, 0), (3, 0)], [(2, 1), (3, 1)], [(0, 2), (0, 3)], [(1, 2), (1, 3)], [(2, 2), (3, 2)], [(2, 3)], [(3, 3)]],
+        )
+        gather(0, 0, E)
         round_and_quantise(1)
-        w1s_late = sbuf([P, G * S * H], U8, "late_scales", "raw10")
-        load_scale_rows(w1s_late[:], w1_rows[G * S : 2 * G * S], H)
-        gather(1, 0)
+        w1s.append(sbuf([P, 2 * S * H], U8, "w1s2", "raw1"))
+        load_scale_rows(w1s[2][:], w1_rows[EARLY * S :], H)
+        gather(1, 0, EARLY)
         round_and_quantise(2)
-
-        w1w_late = sbuf([P, G * S * 2 * H], U8, "late_words", "raw20")[:]
-        load_w1_expert(w1w_late, G, 0, 1)
-        load_w1_pass(w1w_late, 1, 0, 1)
-        load_w1_pass(w1w_late, 1, 1)
-        for e in range(G, E - 1):
-            load_w1_expert(w1w_late, e, 2, S)
-        load_w1_expert(w1w_late, E - 1, 2, LAST)
-        load_w1_expert(w1w_late, E - 1, LAST, S)
-        gather(2, 0)
+        w1_late = sbuf([P, (E - EARLY) * S * PIECE], U8, "w1_late", "raw2")
+        load_w1_all(w1_late, [load for e in range(EARLY, E) for load in ([(e, 0), (e, 1)], [(e, 2)], [(e, 3)])])
+        gather(2, 0, EARLY)
         round_and_quantise(LAST)
 
-        w2_both = sbuf([P, 3 * E * N], U8, "w2_both", "raw30")
+        w2_both = sbuf([P, 3 * E * N], U8, "w2_both", "raw3")
         w2s = w2_both[:, 0 : E * N]
         w2w = w2_both[:, E * N :]
-
-        def load_w2(a, b):
-            nc.sync.dma_start(
-                out=w2w.bitcast(I32).rearrange("p (e n) -> p e n", e=E)[:, a:b, :],
-                in_=w2_words.rearrange("e s p n -> p (e s) n").bitcast(I32)[:, a:b, :],
-            )
-
-        load_w2(0, E - 1)
+        nc.sync.dma_start(
+            out=w2w.bitcast(I32).rearrange("p (e n) -> p e n", e=E), in_=w2_words.rearrange("e s p n -> p (e s) n").bitcast(I32)
+        )
         load_scale_rows(w2s, w2_scales.rearrange("e s q n -> (e s) q n"), N)
-        load_w2(E - 1, E)
 
-        word_pair = sbuf([P, 2 * G * C], U32, "word_pair", "rounded3a")
-        scale_pair = sbuf([P, 2 * G * C], U8, "scale_pair", "rounded3b")
+        late = C * (E - EARLY)
+        word_pair = sbuf([P, 2 * late], U32, "word_pair", "rounded3a")
+        scale_pair = sbuf([P, 2 * late], U8, "scale_pair", "rounded3b")
+        gather(LAST, 0, 2)
+        gather(LAST, 2, EARLY)
         for s in (1, 2):
-            slot_words[s, 1] = word_pair[:, (s - 1) * G * C : s * G * C]
-            slot_scales[s, 1] = scale_pair[:, (s - 1) * G * C : s * G * C]
-        gather(LAST, 0, 0, C)
-        gather(LAST, 0, C, G * C)
-        gather(1, 1)
-        gather(2, 1)
-        for u in range(G):
-            gather(LAST, 1, C * u, C * (u + 1))
+            gather(s, EARLY, E, word_pair[:, (s - 1) * late : s * late], scale_pair[:, (s - 1) * late : s * late])
+        for e in range(EARLY, E):
+            gather(LAST, e, e + 1)
 
-        def first_layer(e, passes):
-            g, u = divmod(e, G)
-            w1w = (w1w_early, w1w_late)[g]
-            w1s = (w1s_early, w1s_late)[g]
-            for s in passes:
-                a = S * u + s
-                nc.tensor.matmul_mx(
-                    out=bank[e][:],
-                    lhsT=slot_words[s, g][:, C * u : C * (u + 1)].bitcast(E4M3),
-                    lhsT_scale=slot_scales[s, g][:, C * u : C * (u + 1)],
-                    rhs=w1w[:, 2 * H * a : 2 * H * (a + 1)].bitcast(E2M1),
-                    rhs_scale=w1s[:, H * a : H * (a + 1)],
-                    start=(s == 0),
-                    stop=(s == LAST),
-                )
-            if LAST in passes:
+        def first_layer(e, s):
+            plane, u = w1s[e // 2], e % 2
+            nc.tensor.matmul_mx(
+                out=bank[e][:],
+                lhsT=slot_words[s, e].bitcast(E4M3),
+                lhsT_scale=slot_scales[s, e],
+                rhs=piece[e, s].bitcast(E2M1),
+                rhs_scale=plane[:, H * (S * u + s) : H * (S * u + s + 1)],
+                start=(s == 0),
+                stop=(s == LAST),
+            )
+            if s == LAST:
                 nc.scalar.activation(
                     hidden[e][:].rearrange("r (half p d) -> r half p d", half=2, d=2),
                     bank[e][:].rearrange("r (p half d) -> r half p d", half=2, d=2),
                     GELU,
                 )
 
-        def turn(e, identity, engine_copy):
+        def turn(e, target, identity):
             pairs = hidden[e][:].bitcast(F32)
             for half in range(2):
-                nc.tensor.transpose(bank[e][:, C * half : C * (half + 1)], pairs[:, P * half : P * (half + 1)], identity[:])
+                nc.tensor.transpose(target[:, C * half : C * (half + 1)], pairs[:, P * half : P * (half + 1)], identity[:])
+
+        def copy_turned(engine_copy, hturned, source):
             engine_copy(
-                hturned[e][:].rearrange("p c t -> p (c t)").bitcast(F32).rearrange("p (c half) -> p c half", half=2),
-                bank[e][:, 0 : 2 * C].rearrange("p (half c) -> p c half", half=2),
-            )
-            nc.vector.quantize_mx(out=hwords[e][:].bitcast(E4M3), scales=hscales[e][:], in_=hturned[e][:].rearrange("p c t -> p (c t)"))
-
-        def second_layer(e, v, target):
-            nc.tensor.matmul_mx(
-                out=target,
-                lhsT=w2w[:, 2 * N * e + 2 * P * v : 2 * N * e + 2 * P * (v + 1)].bitcast(E2M1),
-                lhsT_scale=w2s[:, N * e + P * v : N * e + P * (v + 1)],
-                rhs=hwords[e][:].bitcast(E4M3),
-                rhs_scale=hscales[e][:],
-                start=True,
-                stop=True,
+                hturned.bitcast(F32).rearrange("p (e c half) -> p e c half", c=C, half=2),
+                source.rearrange("p (e half c) -> p e c half", c=C, half=2),
             )
 
-        for s in range(S):
-            for e in range(G):
-                first_layer(e, (s,))
-        for s in range(2):
-            for e in range(G, E):
-                first_layer(e, (s,))
-        for e in range(G, E):
-            first_layer(e, (2, LAST))
+        hwords = {}
+        hscales = {}
 
-        ident_mid = sbuf([P, P], F32, "ident_mid", "slot_words01")
-        ident_end = sbuf([P, P], F32, "ident_end", "slot_words31")
-        turn(0, ident, nc.scalar.copy)
-        turn(1, ident, nc.scalar.copy)
-        nc.scalar.copy(ident_mid[:], ident[:])
-        turn(2, ident_mid, nc.scalar.copy)
-        nc.vector.tensor_copy(ident_end[:], ident[:])
-        turn(3, ident_end, nc.vector.tensor_copy)
-        turn(4, ident_end, nc.scalar.copy)
-        turn(5, ident, nc.scalar.copy)
+        def quantise_h(first, last, hturned):
+            word_tile = sbuf([P, C * (last - first)], U32, f"hwords{first}")
+            scale_tile = sbuf([P, C * (last - first)], U8, f"hscales{first}")
+            nc.vector.quantize_mx(out=word_tile[:].bitcast(E4M3), scales=scale_tile[:], in_=hturned)
+            for e in range(first, last):
+                hwords[e] = word_tile[:, C * (e - first) : C * (e - first + 1)]
+                hscales[e] = scale_tile[:, C * (e - first) : C * (e - first + 1)]
 
-        copies = (nc.vector.tensor_copy, nc.scalar.copy)
-        for a, b, targets in ((0, G, early_out), (G, E - 1, bank[0:2]), (E - 1, E, bank[2:4])):
+        def second_layer(first, last, targets, copies):
             for v in range(2):
-                for e in range(a, b):
-                    second_layer(e, v, targets[v][:, C * (e - a) : C * (e - a + 1)])
-                copies[v](result[:, v, :, a:b, :], targets[v][:, 0 : C * (b - a)].rearrange("p (e m u) -> p m e u", e=b - a, m=R))
+                for e in range(first, last):
+                    nc.tensor.matmul_mx(
+                        out=targets[v][:, C * (e - first) : C * (e - first + 1)],
+                        lhsT=w2w[:, 2 * N * e + 2 * P * v : 2 * N * e + 2 * P * (v + 1)].bitcast(E2M1),
+                        lhsT_scale=w2s[:, N * e + P * v : N * e + P * (v + 1)],
+                        rhs=hwords[e].bitcast(E4M3),
+                        rhs_scale=hscales[e],
+                        start=True,
+                        stop=True,
+                    )
+                copies[v](
+                    result[:, v, :, first:last, :],
+                    targets[v][:, 0 : C * (last - first)].rearrange("p (e m u) -> p m e u", e=last - first, m=R),
+                )
 
-        rows_out = out.rearrange("(v p) (m e u) -> v p m e u", v=2, m=R, e=E)
+        for e, s in piece:
+            if e < EARLY:
+                first_layer(e, s)
+
+        hturned_early = sbuf([P, EARLY * H], BF16, "hturned_early")
+        turn(0, bank[2][:, 0 : 2 * C], ident)
+        turn(1, bank[2][:, 2 * C : 4 * C], ident)
+        turn(2, bank[1][:, 0 : 2 * C], ident)
+        turn(3, bank[3][:, 0 : 2 * C], ident)
+        copy_turned(nc.scalar.copy, hturned_early[:, 0 : 2 * H], bank[2][:])
+        copy_turned(nc.scalar.copy, hturned_early[:, 2 * H : 3 * H], bank[1][:, 0 : 2 * C])
+        copy_turned(nc.scalar.copy, hturned_early[:, 3 * H : 4 * H], bank[3][:, 0 : 2 * C])
+
+        for e, s in piece:
+            if e >= EARLY:
+                first_layer(e, s)
+        quantise_h(0, EARLY, hturned_early[:])
+
+        ident_end = sbuf([P, P], F32, "ident_end", f"slot_words{LAST}{E - 1}")
+        nc.vector.tensor_copy(ident_end[:], ident[:])
+        for e, identity, engine_copy in ((4, ident_end, nc.vector.tensor_copy), (5, ident, nc.scalar.copy)):
+            hturned = sbuf([P, H], BF16, f"hturned{e}")
+            turn(e, bank[e][:, 0 : 2 * C], identity)
+            copy_turned(engine_copy, hturned[:], bank[e][:, 0 : 2 * C])
+            quantise_h(e, e + 1, hturned[:])
+
+        second_layer(0, EARLY, bank[6:8], (nc.scalar.copy, nc.scalar.copy))
+        second_layer(4, 5, bank[0:2], (nc.vector.tensor_copy, nc.vector.tensor_copy))
+        second_layer(5, 6, bank[2:4], (nc.vector.tensor_copy, nc.scalar.copy))
+
+        rows_out = out.rearrange("(v p) c -> v p c", v=2)
         for v in range(2):
-            nc.sync.dma_start(
-                out=rows_out[v].rearrange("p m e u -> p m (e u)"),
-                in_=result[:, v, :, :, :].rearrange("p m e u -> p m (e u)"),
-            )
+            nc.sync.dma_start(out=rows_out[v], in_=result[:, v, :, :, :].rearrange("p m e u -> p (m e u)"))

@@ -257,6 +257,9 @@ def tile_moe_eps_mlp_gelu_kernel(tc, xT, w1_words, w1_scales, w2_words, w2_scale
         second_layer(4, 5, bank[0:2], (nc.vector.tensor_copy, nc.vector.tensor_copy))
         second_layer(5, 6, bank[2:4], (nc.vector.tensor_copy, nc.scalar.copy))
 
-        rows_out = out.rearrange("(v p) c -> v p c", v=2)
-        for v in range(2):
-            nc.sync.dma_start(out=rows_out[v], in_=result[:, v, :, :, :].rearrange("p m e u -> p (m e u)"))
+        rows_out = out.rearrange("(v p) (m c) -> v p m c", v=2, m=R)
+        for first, last in ((0, EARLY), (EARLY, E)):
+            for v in range(2):
+                nc.sync.dma_start(
+                    out=rows_out[v][:, :, U * first : U * last], in_=result[:, v, :, first:last, :].rearrange("p m e u -> p m (e u)")
+                )

@@ -148,7 +148,16 @@ def tile_moe_eps_mlp_gelu_kernel(tc, xT, w1_words, w1_scales, w2_words, w2_scale
         gather(1, 0, EARLY)
         round_and_quantise(2)
         w1_late = sbuf([P, (E - EARLY) * S * PIECE], U8, "w1_late", "raw2")
-        load_w1_all(w1_late, [load for e in range(EARLY, E) for load in ([(e, 0), (e, 1)], [(e, 2)], [(e, 3)])])
+        load_w1_all(w1_late, [[(4, 0), (4, 1)], [(4, 2), (4, 3)], [(5, 0), (5, 1)]])
+        half_piece = {(s, h): piece[5, s][:, H * h : H * (h + 1)] for s in range(2) for h in range(2)}
+        for h in range(2):
+            place = (6 + h) * PIECE
+            nc.sync.dma_start(
+                out=w1_late[:, place : place + PIECE].bitcast(I32).rearrange("p (a n) -> p a n", a=2),
+                in_=w1_pieces[:, S * 5 + 2 : S * 5 + 4, H // 4 * h : H // 4 * (h + 1)],
+            )
+            for s in (2, LAST):
+                half_piece[s, h] = w1_late[:, place + H * (s - 2) : place + H * (s - 1)]
         gather(2, 0, EARLY)
         round_and_quantise(LAST)
 
@@ -185,6 +194,23 @@ def tile_moe_eps_mlp_gelu_kernel(tc, xT, w1_words, w1_scales, w2_words, w2_scale
                 nc.scalar.activation(
                     hidden[e][:].rearrange("r (half p d) -> r half p d", half=2, d=2),
                     bank[e][:].rearrange("r (p half d) -> r half p d", half=2, d=2),
+                    GELU,
+                )
+
+        def last_expert_half(h, s, target):
+            nc.tensor.matmul_mx(
+                out=target[:, 0 : H // 2],
+                lhsT=slot_words[s, 5].bitcast(E4M3),
+                lhsT_scale=slot_scales[s, 5],
+                rhs=half_piece[s, h].bitcast(E2M1),
+                rhs_scale=w1s[2][:, H * (S + s) + H // 2 * h : H * (S + s) + H // 2 * (h + 1)],
+                start=(s == 0),
+                stop=(s == LAST),
+            )
+            if s == LAST:
+                nc.scalar.activation(
+                    hidden[5][:].rearrange("r (half p d) -> r half p d", half=2, d=2)[:, :, P // 2 * h : P // 2 * (h + 1), :],
+                    target[:, 0 : H // 2].rearrange("r (p half d) -> r half p d", half=2, d=2),
                     GELU,
                 )
 
@@ -240,26 +266,27 @@ def tile_moe_eps_mlp_gelu_kernel(tc, xT, w1_words, w1_scales, w2_words, w2_scale
         copy_turned(nc.scalar.copy, hturned_early[:, 2 * H : 3 * H], bank[1][:, 0 : 2 * C])
         copy_turned(nc.scalar.copy, hturned_early[:, 3 * H : 4 * H], bank[3][:, 0 : 2 * C])
 
-        for e, s in piece:
-            if e >= EARLY:
-                first_layer(e, s)
+        for s in range(S):
+            first_layer(4, s)
+        halves = (bank[5], bank[0])
+        for h, s in [(h, s) for s in range(2) for h in range(2)] + [(h, s) for h in range(2) for s in (2, LAST)]:
+            last_expert_half(h, s, halves[h])
         quantise_h(0, EARLY, hturned_early[:])
 
-        ident_end = sbuf([P, P], F32, "ident_end", f"slot_words{LAST}{E - 1}")
-        nc.vector.tensor_copy(ident_end[:], ident[:])
-        for e, identity, engine_copy in ((4, ident_end, nc.vector.tensor_copy), (5, ident, nc.scalar.copy)):
-            hturned = sbuf([P, H], BF16, f"hturned{e}")
-            turn(e, bank[e][:, 0 : 2 * C], identity)
-            copy_turned(engine_copy, hturned[:], bank[e][:, 0 : 2 * C])
-            quantise_h(e, e + 1, hturned[:])
+        hturned = {e: sbuf([P, H], BF16, f"hturned{e}") for e in (4, 5)}
+        for e, target in ((5, halves[0]), (4, halves[1])):
+            turn(e, target[:, 0 : 2 * C], ident)
+        for e, target, engine_copy in ((5, halves[0], nc.scalar.copy), (4, halves[1], nc.vector.tensor_copy)):
+            copy_turned(engine_copy, hturned[e][:], target[:, 0 : 2 * C])
+        for e in (5, 4):
+            quantise_h(e, e + 1, hturned[e][:])
 
         second_layer(0, EARLY, bank[6:8], (nc.scalar.copy, nc.scalar.copy))
-        second_layer(4, 5, bank[0:2], (nc.vector.tensor_copy, nc.vector.tensor_copy))
-        second_layer(5, 6, bank[2:4], (nc.vector.tensor_copy, nc.scalar.copy))
+        second_layer(EARLY, E, bank[2:4], (nc.vector.tensor_copy, nc.scalar.copy))
 
         rows_out = out.rearrange("(v p) (m c) -> v p m c", v=2, m=R)
         for first, last in ((0, EARLY), (EARLY, E)):
-            for v in range(2):
-                nc.sync.dma_start(
-                    out=rows_out[v][:, :, U * first : U * last], in_=result[:, v, :, first:last, :].rearrange("p m e u -> p m (e u)")
-                )
+            nc.sync.dma_start(
+                out=rows_out[0][:, :, U * first : U * last], in_=result[:, 0, :, first:last, :].rearrange("p m e u -> p m (e u)")
+            )
+        nc.sync.dma_start(out=out[P:, :], in_=result[:, 1, :, :, :].rearrange("p m e u -> p (m e u)"))

@@ -139,7 +139,7 @@ def tile_moe_eps_mlp_gelu_kernel(tc, xT, w1_words, w1_scales, w2_words, w2_scale
         w1_early = sbuf([P, 12 * PIECE], U8, "w1_early", "rounded0a")
         load_w1_all(
             w1_early,
-            [[(2, 0), (3, 0)], [(2, 1), (3, 1)], [(0, 2), (0, 3)], [(1, 2), (1, 3)], [(2, 2), (3, 2)], [(2, 3)], [(3, 3)]],
+            [[(2, 0), (3, 0)], [(2, 1), (3, 1)], [(0, 2), (0, 3)], [(1, 2), (1, 3)], [(2, 2)], [(2, 3), (3, 2)], [(3, 3)]],
         )
         gather(0, 0, E)
         round_and_quantise(1)
@@ -274,15 +274,16 @@ def tile_moe_eps_mlp_gelu_kernel(tc, xT, w1_words, w1_scales, w2_words, w2_scale
         quantise_h(0, EARLY, hturned_early[:])
 
         hturned = {e: sbuf([P, H], BF16, f"hturned{e}") for e in (4, 5)}
-        for e, target in ((5, halves[0]), (4, halves[1])):
-            turn(e, target[:, 0 : 2 * C], ident)
-        for e, target, engine_copy in ((5, halves[0], nc.scalar.copy), (4, halves[1], nc.vector.tensor_copy)):
-            copy_turned(engine_copy, hturned[e][:], target[:, 0 : 2 * C])
-        for e in (5, 4):
+        ident_end = sbuf([P, P], F32, "ident_end", f"slot_words{LAST}{E - 1}")
+        nc.vector.tensor_copy(ident_end[:], ident[:])
+        for e, identity, engine_copy in ((4, ident_end, nc.vector.tensor_copy), (5, ident, nc.scalar.copy)):
+            turn(e, bank[e][:, 0 : 2 * C], identity)
+            copy_turned(engine_copy, hturned[e][:], bank[e][:, 0 : 2 * C])
             quantise_h(e, e + 1, hturned[e][:])
 
-        second_layer(0, EARLY, bank[6:8], (nc.scalar.copy, nc.scalar.copy))
-        second_layer(EARLY, E, bank[2:4], (nc.vector.tensor_copy, nc.scalar.copy))
+        second_layer(0, EARLY, bank[6:8], (nc.scalar.copy, nc.vector.tensor_copy))
+        second_layer(4, 5, (bank[1], bank[4]), (nc.scalar.copy, nc.scalar.copy))
+        second_layer(5, 6, bank[2:4], (nc.scalar.copy, nc.vector.tensor_copy))
 
         rows_out = out.rearrange("(v p) (m c) -> v p m c", v=2, m=R)
         for first, last in ((0, EARLY), (EARLY, E)):

@@ -173,7 +173,8 @@ def tile_moe_eps_mlp_gelu_kernel(tc, xT, w1_words, w1_scales, w2_words, w2_scale
         word_pair = sbuf([P, 2 * late], U32, "word_pair", "rounded3a")
         scale_pair = sbuf([P, 2 * late], U8, "scale_pair", "rounded3b")
         gather(LAST, 0, 2)
-        gather(LAST, 2, EARLY)
+        gather(LAST, 2, 3)
+        gather(LAST, 3, EARLY)
         for s in (1, 2):
             gather(s, EARLY, E, word_pair[:, (s - 1) * late : s * late], scale_pair[:, (s - 1) * late : s * late])
         for e in range(EARLY, E):

@@ -37,7 +37,8 @@ def tile_moe_eps_mlp_gelu_kernel(tc, xT, w1_words, w1_scales, w2_words, w2_scale
             return keep.tile(shape, dtype, name=name, tag=tag or name, align_bytes=256)
 
         offsets = keep.tile([P, E * C // 16], U16, name="offsets")
-        raw = [placed.tile([P, 4, T], F32, name="raw0", offset=0, align_bytes=256)] + [sbuf([P, 4, T], F32, f"raw{s}") for s in range(1, S)]
+        raw = [placed.tile([P, 4, T], F32, name="raw0", offset=0, align_bytes=256)] + [sbuf([P, 4, T], F32, f"raw{s}") for s in (1, LAST)]
+        raw.insert(2, placed.tile([P, 4, T], F32, name="raw2", offset=16 * T, align_bytes=256))
         rounded = {}
         for s in range(S):
             rounded[s, 0] = sbuf([P, WIDE, 4], BF16, f"rounded{s}a")
@@ -147,17 +148,17 @@ def tile_moe_eps_mlp_gelu_kernel(tc, xT, w1_words, w1_scales, w2_words, w2_scale
         load_scale_rows(w1s[2][:], w1_rows[EARLY * S :], H)
         gather(1, 0, EARLY)
         round_and_quantise(2)
-        w1_late = sbuf([P, (E - EARLY) * S * PIECE], U8, "w1_late", "raw2")
+        w1_late = placed.tile([P, 6 * PIECE], U8, name="w1_late", offset=16 * T, align_bytes=256)
+        last_halves = [placed.tile([P, PIECE], U8, name=f"last_half{h}", offset=16 * T + (6 + h) * PIECE, align_bytes=256) for h in range(2)]
         load_w1_all(w1_late, [[(4, 0), (4, 1)], [(4, 2), (4, 3)], [(5, 0), (5, 1)]])
         half_piece = {(s, h): piece[5, s][:, H * h : H * (h + 1)] for s in range(2) for h in range(2)}
         for h in range(2):
-            place = (6 + h) * PIECE
             nc.sync.dma_start(
-                out=w1_late[:, place : place + PIECE].bitcast(I32).rearrange("p (a n) -> p a n", a=2),
+                out=last_halves[h][:].bitcast(I32).rearrange("p (a n) -> p a n", a=2),
                 in_=w1_pieces[:, S * 5 + 2 : S * 5 + 4, H // 4 * h : H // 4 * (h + 1)],
             )
             for s in (2, LAST):
-                half_piece[s, h] = w1_late[:, place + H * (s - 2) : place + H * (s - 1)]
+                half_piece[s, h] = last_halves[h][:, H * (s - 2) : H * (s - 1)]
         gather(2, 0, EARLY)
         round_and_quantise(LAST)
 
@@ -173,8 +174,7 @@ def tile_moe_eps_mlp_gelu_kernel(tc, xT, w1_words, w1_scales, w2_words, w2_scale
         word_pair = sbuf([P, 2 * late], U32, "word_pair", "rounded3a")
         scale_pair = sbuf([P, 2 * late], U8, "scale_pair", "rounded3b")
         gather(LAST, 0, 2)
-        gather(LAST, 2, 3)
-        gather(LAST, 3, EARLY)
+        gather(LAST, 2, EARLY)
         for s in (1, 2):
             gather(s, EARLY, E, word_pair[:, (s - 1) * late : s * late], scale_pair[:, (s - 1) * late : s * late])
         for e in range(EARLY, E):
@@ -275,7 +275,7 @@ def tile_moe_eps_mlp_gelu_kernel(tc, xT, w1_words, w1_scales, w2_words, w2_scale
         quantise_h(0, EARLY, hturned_early[:])
 
         hturned = {e: sbuf([P, H], BF16, f"hturned{e}") for e in (4, 5)}
-        ident_end = sbuf([P, P], F32, "ident_end", f"slot_words{LAST}{E - 1}")
+        ident_end = placed.tile([P, P], F32, name="ident_end", offset=16 * T + 6 * PIECE, align_bytes=256)
         nc.vector.tensor_copy(ident_end[:], ident[:])
         for e, identity, engine_copy in ((4, ident_end, nc.vector.tensor_copy), (5, ident, nc.scalar.copy)):
             turn(e, bank[e][:, 0 : 2 * C], identity)
@@ -283,7 +283,7 @@ def tile_moe_eps_mlp_gelu_kernel(tc, xT, w1_words, w1_scales, w2_words, w2_scale
             quantise_h(e, e + 1, hturned[e][:])
 
         second_layer(0, EARLY, bank[6:8], (nc.scalar.copy, nc.vector.tensor_copy))
-        second_layer(4, 5, (bank[1], bank[4]), (nc.scalar.copy, nc.scalar.copy))
+        second_layer(4, 5, (bank[1], bank[4]), (nc.scalar.copy, nc.vector.tensor_copy))
         second_layer(5, 6, bank[2:4], (nc.scalar.copy, nc.vector.tensor_copy))
 
         rows_out = out.rearrange("(v p) (m c) -> v p m c", v=2, m=R)

@@ -19,7 +19,7 @@ S = K // 512
 U = C // R
 EARLY = 4
 LAST = S - 1
-SHARE = 416
+SHARE = 432
 WIDE = 512
 PIECE = 2 * H
 WINDOW = (1024, 704, 704, 704)
@@ -37,7 +37,8 @@ def tile_moe_eps_mlp_gelu_kernel(tc, xT, w1_words, w1_scales, w2_words, w2_scale
             return keep.tile(shape, dtype, name=name, tag=tag or name, align_bytes=256)
 
         offsets = keep.tile([P, E * C // 16], U16, name="offsets")
-        raw = [placed.tile([P, 4, T], F32, name="raw0", offset=0, align_bytes=256)] + [sbuf([P, 4, T], F32, f"raw{s}") for s in (1, LAST)]
+        first_rows = [placed.tile([P, 2, T], F32, name=f"raw0{j}", offset=8 * T * j, align_bytes=256) for j in range(2)]
+        raw = [None] + [sbuf([P, 4, T], F32, f"raw{s}") for s in (1, LAST)]
         raw.insert(2, placed.tile([P, 4, T], F32, name="raw2", offset=16 * T, align_bytes=256))
         rounded = {}
         for s in range(S):
@@ -108,34 +109,39 @@ def tile_moe_eps_mlp_gelu_kernel(tc, xT, w1_words, w1_scales, w2_words, w2_scale
         slot_words = {}
         slot_scales = {}
 
+        def gather_one(slots, tables, s, first, last, target):
+            nc.vector.tensor_copy(target, tables[s][:].indirect(offsets[:, C * first // 16 : C * last // 16]))
+            for e in range(first, last):
+                slots[s, e] = target[:, C * (e - first) : C * (e - first + 1)]
+
         def gather(s, first, last, word_tile=None, scale_tile=None):
             width = C * (last - first)
-            picks = offsets[:, C * first // 16 : C * last // 16]
             if word_tile is None:
                 word_tile = sbuf([P, width], U32, f"slot_words{s}{first}")[:]
                 scale_tile = sbuf([P, width], U8, f"slot_scales{s}{first}")[:]
-            nc.vector.tensor_copy(word_tile, words[s][:].indirect(picks))
-            nc.vector.tensor_copy(scale_tile, scales[s][:].indirect(picks))
-            for e in range(first, last):
-                slot_words[s, e] = word_tile[:, C * (e - first) : C * (e - first + 1)]
-                slot_scales[s, e] = scale_tile[:, C * (e - first) : C * (e - first + 1)]
+            gather_one(slot_words, words, s, first, last, word_tile)
+            gather_one(slot_scales, scales, s, first, last, scale_tile)
 
-        load_x(0)
+        for j in range(2):
+            nc.sync.dma_start(out=first_rows[j][:], in_=xT[0:512, :].rearrange("(p j) w -> p j w", j=4)[:, 2 * j : 2 * j + 2, :])
         nc.sync.dma_start(offsets[:], offs)
         for s in range(1, S):
             load_x(s)
         w1_ahead = sbuf([P, 4 * PIECE], U8, "w1_ahead")
         load_w1_all(w1_ahead, [[(0, s), (1, s)] for s in range(2)])
 
-        cast(nc.vector.tensor_copy, 0, 0, SHARE)
-        cast(nc.scalar.copy, 0, WIDE, T)
-        cast(nc.scalar.copy, 0, SHARE, WIDE)
+        for j in range(2):
+            for engine_copy, a, b in ((nc.vector.tensor_copy, 0, SHARE), (nc.scalar.copy, WIDE, T), (nc.scalar.copy, SHARE, WIDE)):
+                engine_copy(
+                    rounded_view(0, a, b)[:, :, 2 * j : 2 * j + 2].rearrange("p (c i) t -> p c t i", i=4),
+                    first_rows[j][:, :, a:b].rearrange("p t (c i) -> p c t i", i=4),
+                )
         quantise(0, WIDE, T)
         quantise(0, 0, WIDE)
 
         w1s = []
         for pair in range(2):
-            w1s.append(placed.tile([P, 2 * S * H], U8, name=f"w1s{pair}", offset=2 * S * H * pair, align_bytes=256))
+            w1s.append(placed.tile([P, 2 * S * H], U8, name=f"w1s{pair}", offset=8 * T * pair, align_bytes=256))
             load_scale_rows(w1s[pair][:], w1_rows[2 * S * pair : 2 * S * (pair + 1)], H)
         w1_early = sbuf([P, 12 * PIECE], U8, "w1_early", "rounded0a")
         load_w1_all(
@@ -177,8 +183,9 @@ def tile_moe_eps_mlp_gelu_kernel(tc, xT, w1_words, w1_scales, w2_words, w2_scale
         gather(LAST, 2, EARLY)
         for s in (1, 2):
             gather(s, EARLY, E, word_pair[:, (s - 1) * late : s * late], scale_pair[:, (s - 1) * late : s * late])
-        for e in range(EARLY, E):
-            gather(LAST, e, e + 1)
+        gather_one(slot_words, words, LAST, 4, 5, sbuf([P, C], U32, "slot_words34")[:])
+        gather_one(slot_scales, scales, LAST, EARLY, E, sbuf([P, late], U8, "slot_scales34")[:])
+        gather_one(slot_words, words, LAST, 5, 6, sbuf([P, C], U32, "slot_words35")[:])
 
         def first_layer(e, s):
             plane, u = w1s[e // 2], e % 2

@@ -37,9 +37,8 @@ def tile_moe_eps_mlp_gelu_kernel(tc, xT, w1_words, w1_scales, w2_words, w2_scale
             return keep.tile(shape, dtype, name=name, tag=tag or name, align_bytes=256)
 
         offsets = keep.tile([P, E * C // 16], U16, name="offsets")
-        first_rows = [placed.tile([P, 2, T], F32, name=f"raw0{j}", offset=8 * T * j, align_bytes=256) for j in range(2)]
-        raw = [None] + [sbuf([P, 4, T], F32, f"raw{s}") for s in (1, LAST)]
-        raw.insert(2, placed.tile([P, 4, T], F32, name="raw2", offset=16 * T, align_bytes=256))
+        first_rows = [sbuf([P, 2, T], F32, f"raw0{j}") for j in range(2)]
+        raw = [None] + [sbuf([P, 4, T], F32, f"raw{s}") for s in range(1, S)]
         rounded = {}
         for s in range(S):
             rounded[s, 0] = sbuf([P, WIDE, 4], BF16, f"rounded{s}a")
@@ -50,6 +49,13 @@ def tile_moe_eps_mlp_gelu_kernel(tc, xT, w1_words, w1_scales, w2_words, w2_scale
         ident = keep.tile([P, P], F32, name="ident")
         result = sbuf([P, 2, R, E, U], F32, "result")
         bank = [psum.tile([P, H], F32, name=f"bank{b}") for b in range(8)]
+        plane_early = sbuf([P, EARLY * S * H], U8, "plane_early")
+        plane_late = sbuf([P, (E - EARLY) * S * H], U8, "plane_late")
+        w1_early = sbuf([P, EARLY * S * PIECE], U8, "w1_early")
+        w1_late = sbuf([P, 6 * PIECE], U8, "w1_late")
+        last_halves = [placed.tile([P, PIECE], U8, name=f"last_half{h}", offset=h * PIECE, align_bytes=256) for h in range(2)]
+        w2s = sbuf([P, E * N], U8, "w2s")[:]
+        w2w = sbuf([P, 2 * E * N], U8, "w2w")[:]
 
         for s in range(S):
             nc.vector.memset(scales[s][:].bitcast(I32), 0)
@@ -70,6 +76,15 @@ def tile_moe_eps_mlp_gelu_kernel(tc, xT, w1_words, w1_scales, w2_words, w2_scale
         w1_rows = w1_scales.rearrange("e s q i -> (e s) q i")
         piece = {}
 
+        def load_early_rows(first, last):
+            for j in range(first, last):
+                q = 8 * (j % 2) + j // 2
+                part = 32 * (q // 4) + q % 4
+                nc.sync.dma_start(
+                    out=plane_early[part : part + 1].bitcast(I32).rearrange("q (a i) -> q a i", i=H // 4),
+                    in_=w1_rows[0 : EARLY * S, q : q + 1, :].rearrange("a q i -> q a i").bitcast(I32),
+                )
+
         def load_w1(tile, place, pieces):
             at = [S * e + s for e, s in pieces]
             step = at[1] - at[0] if len(at) > 1 else 1
@@ -85,6 +100,35 @@ def tile_moe_eps_mlp_gelu_kernel(tc, xT, w1_words, w1_scales, w2_words, w2_scale
             place = 0
             for pieces in loads:
                 place = load_w1(tile, place, pieces)
+
+        for j in range(2):
+            nc.sync.dma_start(out=first_rows[j][:], in_=xT[0:512, :].rearrange("(p j) w -> p j w", j=4)[:, 2 * j : 2 * j + 2, :])
+        nc.sync.dma_start(offsets[:], offs)
+        load_x(1)
+        load_early_rows(0, 6)
+        load_x(2)
+        load_early_rows(6, 12)
+        load_x(3)
+        load_early_rows(12, 16)
+        early = range(EARLY)
+        load_w1_all(
+            w1_early,
+            [[(0, 0), (1, 0)], [(2, 0), (3, 0)], [(e, 1) for e in early], [(e, 2) for e in early], [(0, 3), (1, 3)], [(2, 3)], [(3, 3)]],
+        )
+        load_scale_rows(plane_late[:], w1_rows[EARLY * S :], H)
+        load_w1_all(w1_late, [[(4, 0), (4, 1)], [(4, 2), (4, 3)], [(5, 0), (5, 1)]])
+        half_piece = {(s, h): piece[5, s][:, H * h : H * (h + 1)] for s in range(2) for h in range(2)}
+        for h in range(2):
+            nc.sync.dma_start(
+                out=last_halves[h][:].bitcast(I32).rearrange("p (a n) -> p a n", a=2),
+                in_=w1_pieces[:, S * 5 + 2 : S * 5 + 4, H // 4 * h : H // 4 * (h + 1)],
+            )
+            for s in (2, LAST):
+                half_piece[s, h] = last_halves[h][:, H * (s - 2) : H * (s - 1)]
+        nc.sync.dma_start(
+            out=w2w.bitcast(I32).rearrange("p (e n) -> p e n", e=E), in_=w2_words.rearrange("e s p n -> p (e s) n").bitcast(I32)
+        )
+        load_scale_rows(w2s, w2_scales.rearrange("e s q n -> (e s) q n"), N)
 
         def rounded_view(s, a, b):
             return rounded[s, 0][:, a:b, :] if b <= WIDE else rounded[s, 1][:, a - WIDE : b - WIDE, :]
@@ -123,14 +167,6 @@ def tile_moe_eps_mlp_gelu_kernel(tc, xT, w1_words, w1_scales, w2_words, w2_scale
             gather_one(slot_scales, scales, s, first, last, scale_tile)
 
         for j in range(2):
-            nc.sync.dma_start(out=first_rows[j][:], in_=xT[0:512, :].rearrange("(p j) w -> p j w", j=4)[:, 2 * j : 2 * j + 2, :])
-        nc.sync.dma_start(offsets[:], offs)
-        for s in range(1, S):
-            load_x(s)
-        w1_ahead = sbuf([P, 4 * PIECE], U8, "w1_ahead")
-        load_w1_all(w1_ahead, [[(0, s), (1, s)] for s in range(2)])
-
-        for j in range(2):
             for engine_copy, a, b in ((nc.vector.tensor_copy, 0, SHARE), (nc.scalar.copy, WIDE, T), (nc.scalar.copy, SHARE, WIDE)):
                 engine_copy(
                     rounded_view(0, a, b)[:, :, 2 * j : 2 * j + 2].rearrange("p (c i) t -> p c t i", i=4),
@@ -138,43 +174,12 @@ def tile_moe_eps_mlp_gelu_kernel(tc, xT, w1_words, w1_scales, w2_words, w2_scale
                 )
         quantise(0, WIDE, T)
         quantise(0, 0, WIDE)
-
-        w1s = []
-        for pair in range(2):
-            w1s.append(placed.tile([P, 2 * S * H], U8, name=f"w1s{pair}", offset=8 * T * pair, align_bytes=256))
-            load_scale_rows(w1s[pair][:], w1_rows[2 * S * pair : 2 * S * (pair + 1)], H)
-        w1_early = sbuf([P, 12 * PIECE], U8, "w1_early", "rounded0a")
-        load_w1_all(
-            w1_early,
-            [[(2, 0), (3, 0)], [(2, 1), (3, 1)], [(0, 2), (0, 3)], [(1, 2), (1, 3)], [(2, 2)], [(2, 3), (3, 2)], [(3, 3)]],
-        )
         gather(0, 0, E)
         round_and_quantise(1)
-        w1s.append(sbuf([P, 2 * S * H], U8, "w1s2", "raw1"))
-        load_scale_rows(w1s[2][:], w1_rows[EARLY * S :], H)
         gather(1, 0, EARLY)
         round_and_quantise(2)
-        w1_late = placed.tile([P, 6 * PIECE], U8, name="w1_late", offset=16 * T, align_bytes=256)
-        last_halves = [placed.tile([P, PIECE], U8, name=f"last_half{h}", offset=16 * T + (6 + h) * PIECE, align_bytes=256) for h in range(2)]
-        load_w1_all(w1_late, [[(4, 0), (4, 1)], [(4, 2), (4, 3)], [(5, 0), (5, 1)]])
-        half_piece = {(s, h): piece[5, s][:, H * h : H * (h + 1)] for s in range(2) for h in range(2)}
-        for h in range(2):
-            nc.sync.dma_start(
-                out=last_halves[h][:].bitcast(I32).rearrange("p (a n) -> p a n", a=2),
-                in_=w1_pieces[:, S * 5 + 2 : S * 5 + 4, H // 4 * h : H // 4 * (h + 1)],
-            )
-            for s in (2, LAST):
-                half_piece[s, h] = last_halves[h][:, H * (s - 2) : H * (s - 1)]
         gather(2, 0, EARLY)
         round_and_quantise(LAST)
-
-        w2_both = sbuf([P, 3 * E * N], U8, "w2_both", "raw3")
-        w2s = w2_both[:, 0 : E * N]
-        w2w = w2_both[:, E * N :]
-        nc.sync.dma_start(
-            out=w2w.bitcast(I32).rearrange("p (e n) -> p e n", e=E), in_=w2_words.rearrange("e s p n -> p (e s) n").bitcast(I32)
-        )
-        load_scale_rows(w2s, w2_scales.rearrange("e s q n -> (e s) q n"), N)
 
         late = C * (E - EARLY)
         word_pair = sbuf([P, 2 * late], U32, "word_pair", "rounded3a")
@@ -188,7 +193,7 @@ def tile_moe_eps_mlp_gelu_kernel(tc, xT, w1_words, w1_scales, w2_words, w2_scale
         gather_one(slot_words, words, LAST, 5, 6, sbuf([P, C], U32, "slot_words35")[:])
 
         def first_layer(e, s):
-            plane, u = w1s[e // 2], e % 2
+            plane, u = (plane_early, e) if e < EARLY else (plane_late, e - EARLY)
             nc.tensor.matmul_mx(
                 out=bank[e][:],
                 lhsT=slot_words[s, e].bitcast(E4M3),
@@ -211,7 +216,7 @@ def tile_moe_eps_mlp_gelu_kernel(tc, xT, w1_words, w1_scales, w2_words, w2_scale
                 lhsT=slot_words[s, 5].bitcast(E4M3),
                 lhsT_scale=slot_scales[s, 5],
                 rhs=half_piece[s, h].bitcast(E2M1),
-                rhs_scale=w1s[2][:, H * (S + s) + H // 2 * h : H * (S + s) + H // 2 * (h + 1)],
+                rhs_scale=plane_late[:, H * (S + s) + H // 2 * h : H * (S + s) + H // 2 * (h + 1)],
                 start=(s == 0),
                 stop=(s == LAST),
             )
@@ -282,7 +287,7 @@ def tile_moe_eps_mlp_gelu_kernel(tc, xT, w1_words, w1_scales, w2_words, w2_scale
         quantise_h(0, EARLY, hturned_early[:])
 
         hturned = {e: sbuf([P, H], BF16, f"hturned{e}") for e in (4, 5)}
-        ident_end = placed.tile([P, P], F32, name="ident_end", offset=16 * T + 6 * PIECE, align_bytes=256)
+        ident_end = placed.tile([P, P], F32, name="ident_end", offset=0, align_bytes=256)
         nc.vector.tensor_copy(ident_end[:], ident[:])
         for e, identity, engine_copy in ((4, ident_end, nc.vector.tensor_copy), (5, ident, nc.scalar.copy)):
             turn(e, bank[e][:, 0 : 2 * C], identity)

@@ -49,8 +49,7 @@ def tile_moe_eps_mlp_gelu_kernel(tc, xT, w1_words, w1_scales, w2_words, w2_scale
         ident = keep.tile([P, P], F32, name="ident")
         result = sbuf([P, 2, R, E, U], F32, "result")
         bank = [psum.tile([P, H], F32, name=f"bank{b}") for b in range(8)]
-        plane_early = sbuf([P, EARLY * S * H], U8, "plane_early")
-        plane_late = sbuf([P, (E - EARLY) * S * H], U8, "plane_late")
+        planes = [sbuf([P, 2 * S * H], U8, f"plane{pair}") for pair in range(E // 2)]
         w1_early = sbuf([P, EARLY * S * PIECE], U8, "w1_early")
         w1_late = sbuf([P, 6 * PIECE], U8, "w1_late")
         last_halves = [placed.tile([P, PIECE], U8, name=f"last_half{h}", offset=h * PIECE, align_bytes=256) for h in range(2)]
@@ -76,15 +75,6 @@ def tile_moe_eps_mlp_gelu_kernel(tc, xT, w1_words, w1_scales, w2_words, w2_scale
         w1_rows = w1_scales.rearrange("e s q i -> (e s) q i")
         piece = {}
 
-        def load_early_rows(first, last):
-            for j in range(first, last):
-                q = 8 * (j % 2) + j // 2
-                part = 32 * (q // 4) + q % 4
-                nc.sync.dma_start(
-                    out=plane_early[part : part + 1].bitcast(I32).rearrange("q (a i) -> q a i", i=H // 4),
-                    in_=w1_rows[0 : EARLY * S, q : q + 1, :].rearrange("a q i -> q a i").bitcast(I32),
-                )
-
         def load_w1(tile, place, pieces):
             at = [S * e + s for e, s in pieces]
             step = at[1] - at[0] if len(at) > 1 else 1
@@ -96,27 +86,26 @@ def tile_moe_eps_mlp_gelu_kernel(tc, xT, w1_words, w1_scales, w2_words, w2_scale
                 piece[key] = tile[:, (place + j) * PIECE : (place + j + 1) * PIECE]
             return place + len(at)
 
-        def load_w1_all(tile, loads):
-            place = 0
+        def load_w1_all(tile, place, loads):
             for pieces in loads:
                 place = load_w1(tile, place, pieces)
+
+        def load_pair_rows(pair):
+            load_scale_rows(planes[pair][:], w1_rows[2 * S * pair : 2 * S * (pair + 1)], H)
 
         for j in range(2):
             nc.sync.dma_start(out=first_rows[j][:], in_=xT[0:512, :].rearrange("(p j) w -> p j w", j=4)[:, 2 * j : 2 * j + 2, :])
         nc.sync.dma_start(offsets[:], offs)
-        load_x(1)
-        load_early_rows(0, 6)
-        load_x(2)
-        load_early_rows(6, 12)
-        load_x(3)
-        load_early_rows(12, 16)
+        for s in range(1, S):
+            load_x(s)
         early = range(EARLY)
-        load_w1_all(
-            w1_early,
-            [[(0, 0), (1, 0)], [(2, 0), (3, 0)], [(e, 1) for e in early], [(e, 2) for e in early], [(0, 3), (1, 3)], [(2, 3)], [(3, 3)]],
-        )
-        load_scale_rows(plane_late[:], w1_rows[EARLY * S :], H)
-        load_w1_all(w1_late, [[(4, 0), (4, 1)], [(4, 2), (4, 3)], [(5, 0), (5, 1)]])
+        load_w1(w1_early, 0, [(e, 0) for e in early])
+        load_pair_rows(0)
+        load_pair_rows(1)
+        load_w1_all(w1_early, EARLY, [[(e, 1) for e in early], [(e, 2) for e in early], [(0, 3), (1, 3)], [(2, 3), (3, 3)]])
+        load_pair_rows(2)
+        load_scale_rows(w2s, w2_scales.rearrange("e s q n -> (e s) q n"), N)
+        load_w1_all(w1_late, 0, [[(4, s) for s in range(S)], [(5, 0), (5, 1)]])
         half_piece = {(s, h): piece[5, s][:, H * h : H * (h + 1)] for s in range(2) for h in range(2)}
         for h in range(2):
             nc.sync.dma_start(
@@ -128,7 +117,6 @@ def tile_moe_eps_mlp_gelu_kernel(tc, xT, w1_words, w1_scales, w2_words, w2_scale
         nc.sync.dma_start(
             out=w2w.bitcast(I32).rearrange("p (e n) -> p e n", e=E), in_=w2_words.rearrange("e s p n -> p (e s) n").bitcast(I32)
         )
-        load_scale_rows(w2s, w2_scales.rearrange("e s q n -> (e s) q n"), N)
 
         def rounded_view(s, a, b):
             return rounded[s, 0][:, a:b, :] if b <= WIDE else rounded[s, 1][:, a - WIDE : b - WIDE, :]
@@ -193,7 +181,7 @@ def tile_moe_eps_mlp_gelu_kernel(tc, xT, w1_words, w1_scales, w2_words, w2_scale
         gather_one(slot_words, words, LAST, 5, 6, sbuf([P, C], U32, "slot_words35")[:])
 
         def first_layer(e, s):
-            plane, u = (plane_early, e) if e < EARLY else (plane_late, e - EARLY)
+            plane, u = planes[e // 2], e % 2
             nc.tensor.matmul_mx(
                 out=bank[e][:],
                 lhsT=slot_words[s, e].bitcast(E4M3),
@@ -216,7 +204,7 @@ def tile_moe_eps_mlp_gelu_kernel(tc, xT, w1_words, w1_scales, w2_words, w2_scale
                 lhsT=slot_words[s, 5].bitcast(E4M3),
                 lhsT_scale=slot_scales[s, 5],
                 rhs=half_piece[s, h].bitcast(E2M1),
-                rhs_scale=plane_late[:, H * (S + s) + H // 2 * h : H * (S + s) + H // 2 * (h + 1)],
+                rhs_scale=planes[2][:, H * (S + s) + H // 2 * h : H * (S + s) + H // 2 * (h + 1)],
                 start=(s == 0),
                 stop=(s == LAST),
             )

@@ -98,14 +98,16 @@ def tile_moe_eps_mlp_gelu_kernel(tc, xT, w1_words, w1_scales, w2_words, w2_scale
         nc.sync.dma_start(offsets[:], offs)
         for s in range(1, S):
             load_x(s)
-        early = range(EARLY)
-        load_w1(w1_early, 0, [(e, 0) for e in early])
+        load_w1_all(w1_early, 0, [[(0, s), (1, s)] for s in range(2)])
         load_pair_rows(0)
         load_pair_rows(1)
-        load_w1_all(w1_early, EARLY, [[(e, 1) for e in early], [(e, 2) for e in early], [(0, 3), (1, 3)], [(2, 3), (3, 3)]])
+        load_w1_all(
+            w1_early,
+            4,
+            [[(2, 0), (3, 0)], [(2, 1), (3, 1)], [(0, 2), (0, 3)], [(1, 2), (1, 3)], [(2, 2)], [(2, 3), (3, 2)], [(3, 3)]],
+        )
         load_pair_rows(2)
-        load_scale_rows(w2s, w2_scales.rearrange("e s q n -> (e s) q n"), N)
-        load_w1_all(w1_late, 0, [[(4, s) for s in range(S)], [(5, 0), (5, 1)]])
+        load_w1_all(w1_late, 0, [[(4, 0), (4, 1)], [(4, 2), (4, 3)], [(5, 0), (5, 1)]])
         half_piece = {(s, h): piece[5, s][:, H * h : H * (h + 1)] for s in range(2) for h in range(2)}
         for h in range(2):
             nc.sync.dma_start(
@@ -117,6 +119,7 @@ def tile_moe_eps_mlp_gelu_kernel(tc, xT, w1_words, w1_scales, w2_words, w2_scale
         nc.sync.dma_start(
             out=w2w.bitcast(I32).rearrange("p (e n) -> p e n", e=E), in_=w2_words.rearrange("e s p n -> p (e s) n").bitcast(I32)
         )
+        load_scale_rows(w2s, w2_scales.rearrange("e s q n -> (e s) q n"), N)
 
         def rounded_view(s, a, b):
             return rounded[s, 0][:, a:b, :] if b <= WIDE else rounded[s, 1][:, a - WIDE : b - WIDE, :]
@@ -166,18 +169,22 @@ def tile_moe_eps_mlp_gelu_kernel(tc, xT, w1_words, w1_scales, w2_words, w2_scale
         round_and_quantise(1)
         gather(1, 0, EARLY)
         round_and_quantise(2)
-        gather(2, 0, EARLY)
+        gather_one(slot_words, words, 2, 0, EARLY, sbuf([P, EARLY * C], U32, "slot_words20")[:])
+        gather_one(slot_scales, scales, 2, 0, 2, sbuf([P, 2 * C], U8, "slot_scales20")[:])
         round_and_quantise(LAST)
+        gather_one(slot_scales, scales, 2, 2, EARLY, sbuf([P, 2 * C], U8, "slot_scales22", "raw3")[:])
 
         late = C * (E - EARLY)
         word_pair = sbuf([P, 2 * late], U32, "word_pair", "rounded3a")
         scale_pair = sbuf([P, 2 * late], U8, "scale_pair", "rounded3b")
         gather(LAST, 0, 2)
         gather(LAST, 2, EARLY)
-        for s in (1, 2):
-            gather(s, EARLY, E, word_pair[:, (s - 1) * late : s * late], scale_pair[:, (s - 1) * late : s * late])
+        gather(1, EARLY, E, word_pair[:, 0:late], scale_pair[:, 0:late])
+        gather_one(slot_scales, scales, 2, EARLY, E, scale_pair[:, late:])
+        gather_one(slot_words, words, 2, 4, 5, word_pair[:, late : late + C])
         gather_one(slot_words, words, LAST, 4, 5, sbuf([P, C], U32, "slot_words34")[:])
         gather_one(slot_scales, scales, LAST, EARLY, E, sbuf([P, late], U8, "slot_scales34")[:])
+        gather_one(slot_words, words, 2, 5, 6, word_pair[:, late + C :])
         gather_one(slot_words, words, LAST, 5, 6, sbuf([P, C], U32, "slot_words35")[:])
 
         def first_layer(e, s):
@@ -237,22 +244,21 @@ def tile_moe_eps_mlp_gelu_kernel(tc, xT, w1_words, w1_scales, w2_words, w2_scale
                 hwords[e] = word_tile[:, C * (e - first) : C * (e - first + 1)]
                 hscales[e] = scale_tile[:, C * (e - first) : C * (e - first + 1)]
 
-        def second_layer(first, last, targets, copies):
-            for v in range(2):
-                for e in range(first, last):
-                    nc.tensor.matmul_mx(
-                        out=targets[v][:, C * (e - first) : C * (e - first + 1)],
-                        lhsT=w2w[:, 2 * N * e + 2 * P * v : 2 * N * e + 2 * P * (v + 1)].bitcast(E2M1),
-                        lhsT_scale=w2s[:, N * e + P * v : N * e + P * (v + 1)],
-                        rhs=hwords[e].bitcast(E4M3),
-                        rhs_scale=hscales[e],
-                        start=True,
-                        stop=True,
-                    )
-                copies[v](
-                    result[:, v, :, first:last, :],
-                    targets[v][:, 0 : C * (last - first)].rearrange("p (e m u) -> p m e u", e=last - first, m=R),
+        def second_layer(v, first, last, target):
+            for e in range(first, last):
+                nc.tensor.matmul_mx(
+                    out=target[:, C * (e - first) : C * (e - first + 1)],
+                    lhsT=w2w[:, 2 * N * e + 2 * P * v : 2 * N * e + 2 * P * (v + 1)].bitcast(E2M1),
+                    lhsT_scale=w2s[:, N * e + P * v : N * e + P * (v + 1)],
+                    rhs=hwords[e].bitcast(E4M3),
+                    rhs_scale=hscales[e],
+                    start=True,
+                    stop=True,
                 )
+            (nc.scalar.copy, nc.vector.tensor_copy)[v](
+                result[:, v, :, first:last, :],
+                target[:, 0 : C * (last - first)].rearrange("p (e m u) -> p m e u", e=last - first, m=R),
+            )
 
         for e, s in piece:
             if e < EARLY:
@@ -282,9 +288,8 @@ def tile_moe_eps_mlp_gelu_kernel(tc, xT, w1_words, w1_scales, w2_words, w2_scale
             copy_turned(engine_copy, hturned[e][:], bank[e][:, 0 : 2 * C])
             quantise_h(e, e + 1, hturned[e][:])
 
-        second_layer(0, EARLY, bank[6:8], (nc.scalar.copy, nc.vector.tensor_copy))
-        second_layer(4, 5, (bank[1], bank[4]), (nc.scalar.copy, nc.vector.tensor_copy))
-        second_layer(5, 6, bank[2:4], (nc.scalar.copy, nc.vector.tensor_copy))
+        for v, first, last, b in ((0, 0, 2, 6), (0, 2, 4, 7), (1, 0, 2, 1), (1, 2, 4, 2), (0, 4, 5, 3), (1, 4, 5, 4), (0, 5, 6, 0), (1, 5, 6, 5)):
+            second_layer(v, first, last, bank[b])
 
         rows_out = out.rearrange("(v p) (m c) -> v p m c", v=2, m=R)
         for first, last in ((0, EARLY), (EARLY, E)):

@@ -52,9 +52,9 @@ def tile_moe_eps_mlp_gelu_kernel(tc, xT, w1_words, w1_scales, w2_words, w2_scale
         planes = [sbuf([P, 2 * S * H], U8, f"plane{pair}") for pair in range(E // 2)]
         w1_early = sbuf([P, EARLY * S * PIECE], U8, "w1_early")
         w1_late = sbuf([P, 6 * PIECE], U8, "w1_late")
-        last_halves = [placed.tile([P, PIECE], U8, name=f"last_half{h}", offset=h * PIECE, align_bytes=256) for h in range(2)]
+        w1_last_first = placed.tile([P, 2 * PIECE], U8, name="w1_last_first", offset=0, align_bytes=256)
         w2s = sbuf([P, E * N], U8, "w2s")[:]
-        w2w = sbuf([P, 2 * E * N], U8, "w2w")[:]
+        w2w = {}
 
         for s in range(S):
             nc.vector.memset(scales[s][:].bitcast(I32), 0)
@@ -107,19 +107,21 @@ def tile_moe_eps_mlp_gelu_kernel(tc, xT, w1_words, w1_scales, w2_words, w2_scale
             [[(2, 0), (3, 0)], [(2, 1), (3, 1)], [(0, 2), (0, 3)], [(1, 2), (1, 3)], [(2, 2)], [(2, 3), (3, 2)], [(3, 3)]],
         )
         load_pair_rows(2)
-        load_w1_all(w1_late, 0, [[(4, 0), (4, 1)], [(4, 2), (4, 3)], [(5, 0), (5, 1)]])
-        half_piece = {(s, h): piece[5, s][:, H * h : H * (h + 1)] for s in range(2) for h in range(2)}
-        for h in range(2):
-            nc.sync.dma_start(
-                out=last_halves[h][:].bitcast(I32).rearrange("p (a n) -> p a n", a=2),
-                in_=w1_pieces[:, S * 5 + 2 : S * 5 + 4, H // 4 * h : H // 4 * (h + 1)],
-            )
-            for s in (2, LAST):
-                half_piece[s, h] = last_halves[h][:, H * (s - 2) : H * (s - 1)]
-        nc.sync.dma_start(
-            out=w2w.bitcast(I32).rearrange("p (e n) -> p e n", e=E), in_=w2_words.rearrange("e s p n -> p (e s) n").bitcast(I32)
-        )
+        load_w1_all(w1_late, 0, [[(4, 0), (4, 1)], [(4, 2), (4, 3)]])
+        load_w1(w1_last_first, 0, [(5, 0), (5, 1)])
+        load_w1(w1_late, 4, [(5, 2), (5, 3)])
+        half_piece = {(s, h): piece[5, s][:, H * h : H * (h + 1)] for s in range(S) for h in range(2)}
+        w2_rows = w2_words.rearrange("e s p n -> p (e s) n").bitcast(I32)
+
+        def load_w2(first, last):
+            tile = sbuf([P, 2 * N * (last - first)], U8, f"w2w{first}")
+            nc.sync.dma_start(out=tile[:].bitcast(I32).rearrange("p (e n) -> p e n", e=last - first), in_=w2_rows[:, first:last, :])
+            for e in range(first, last):
+                w2w[e] = tile[:, 2 * N * (e - first) : 2 * N * (e - first + 1)]
+
+        load_w2(0, EARLY)
         load_scale_rows(w2s, w2_scales.rearrange("e s q n -> (e s) q n"), N)
+        load_w2(EARLY, E)
 
         def rounded_view(s, a, b):
             return rounded[s, 0][:, a:b, :] if b <= WIDE else rounded[s, 1][:, a - WIDE : b - WIDE, :]
@@ -248,7 +250,7 @@ def tile_moe_eps_mlp_gelu_kernel(tc, xT, w1_words, w1_scales, w2_words, w2_scale
             for e in range(first, last):
                 nc.tensor.matmul_mx(
                     out=target[:, C * (e - first) : C * (e - first + 1)],
-                    lhsT=w2w[:, 2 * N * e + 2 * P * v : 2 * N * e + 2 * P * (v + 1)].bitcast(E2M1),
+                    lhsT=w2w[e][:, 2 * P * v : 2 * P * (v + 1)].bitcast(E2M1),
                     lhsT_scale=w2s[:, N * e + P * v : N * e + P * (v + 1)],
                     rhs=hwords[e].bitcast(E4M3),
                     rhs_scale=hscales[e],

from contextlib import ExitStack

import concourse.mybir as mybir
from concourse.masks import make_identity

F32 = mybir.dt.float32
BF16 = mybir.dt.bfloat16
U32 = mybir.dt.uint32
I32 = mybir.dt.int32
U16 = mybir.dt.uint16
U8 = mybir.dt.uint8
E4M3 = mybir.dt.float8_e4m3fn_x4
E2M1 = mybir.dt.float4_e2m1fn_x4
GELU = mybir.ActivationFunctionType.Gelu_apprx_tanh

P = 128
K, T, E, C, H, N, R = 2048, 640, 6, 128, 512, 256, 4
S = K // 512
U = C // R
EARLY = 4
LAST = S - 1
SHARE = 432
WIDE = 512
PIECE = 2 * H
WINDOW = (1024, 704, 704, 704)
FLOPS = 2 * E * C * (K * H + H * N)


def tile_moe_eps_mlp_gelu_kernel(tc, xT, w1_words, w1_scales, w2_words, w2_scales, offs, out):
    nc = tc.nc
    with ExitStack() as ctx:
        keep = ctx.enter_context(tc.tile_pool(name="keep", bufs=1))
        placed = ctx.enter_context(tc.tile_pool(name="placed", bufs=1))
        psum = ctx.enter_context(tc.psum_pool(name="psum", bufs=1))

        def sbuf(shape, dtype, name, tag=None):
            return keep.tile(shape, dtype, name=name, tag=tag or name, align_bytes=256)

        offsets = keep.tile([P, E * C // 16], U16, name="offsets")
        first_rows = [sbuf([P, 2, T], F32, f"raw0{j}") for j in range(2)]
        raw = [None] + [sbuf([P, 4, T], F32, f"raw{s}") for s in range(1, S)]
        rounded = {}
        for s in range(S):
            rounded[s, 0] = sbuf([P, WIDE, 4], BF16, f"rounded{s}a")
            rounded[s, 1] = sbuf([P, T - WIDE, 4], BF16, f"rounded{s}b")
        words = [sbuf([P, WINDOW[s]], U32, f"words{s}") for s in range(S)]
        scales = [sbuf([P, WINDOW[s]], U8, f"scales{s}") for s in range(S)]
        hidden = [sbuf([P, H], BF16, f"hidden{e}") for e in range(E)]
        ident = keep.tile([P, P], F32, name="ident")
        result = sbuf([P, 2, R, E, U], F32, "result")
        bank = [psum.tile([P, H], F32, name=f"bank{b}") for b in range(8)]
        planes = [sbuf([P, 2 * S * H], U8, f"plane{pair}") for pair in range(E // 2)]
        w1_early = sbuf([P, EARLY * S * PIECE], U8, "w1_early")
        w1_late = sbuf([P, 6 * PIECE], U8, "w1_late")
        w1_last_first = placed.tile([P, 2 * PIECE], U8, name="w1_last_first", offset=0, align_bytes=256)
        w2s = sbuf([P, E * N], U8, "w2s")[:]
        w2w = {}

        for s in range(S):
            nc.vector.memset(scales[s][:].bitcast(I32), 0)
            nc.vector.memset(words[s][:, T:].bitcast(I32), 0)
        make_identity(nc, ident[:])

        def load_x(s):
            nc.sync.dma_start(out=raw[s][:], in_=xT[512 * s : 512 * (s + 1), :].rearrange("(p j) w -> p j w", j=4))

        def load_scale_rows(plane, rows, width):
            for r in range(4):
                nc.sync.dma_start(
                    out=plane[r:P:32].bitcast(I32).rearrange("q (a i) -> q a i", i=width // 4),
                    in_=rows[:, r:16:4, :].rearrange("a q i -> q a i").bitcast(I32),
                )

        w1_pieces = w1_words.rearrange("e s p n -> p (e s) n").bitcast(I32)
        w1_rows = w1_scales.rearrange("e s q i -> (e s) q i")
        piece = {}

        def load_w1(tile, place, pieces):
            at = [S * e + s for e, s in pieces]
            step = at[1] - at[0] if len(at) > 1 else 1
            nc.sync.dma_start(
                out=tile[:, place * PIECE : (place + len(at)) * PIECE].bitcast(I32).rearrange("p (a n) -> p a n", a=len(at)),
                in_=w1_pieces[:, at[0] : at[-1] + 1 : step, :],
            )
            for j, key in enumerate(pieces):
                piece[key] = tile[:, (place + j) * PIECE : (place + j + 1) * PIECE]
            return place + len(at)

        def load_w1_all(tile, place, loads):
            for pieces in loads:
                place = load_w1(tile, place, pieces)

        def load_pair_rows(pair):
            load_scale_rows(planes[pair][:], w1_rows[2 * S * pair : 2 * S * (pair + 1)], H)

        for j in range(2):
            nc.sync.dma_start(out=first_rows[j][:], in_=xT[0:512, :].rearrange("(p j) w -> p j w", j=4)[:, 2 * j : 2 * j + 2, :])
        nc.sync.dma_start(offsets[:], offs)
        for s in range(1, S):
            load_x(s)
        load_w1_all(w1_early, 0, [[(0, s), (1, s)] for s in range(2)])
        load_pair_rows(0)
        load_pair_rows(1)
        load_w1_all(
            w1_early,
            4,
            [[(2, 0), (3, 0)], [(2, 1), (3, 1)], [(0, 2), (0, 3)], [(1, 2), (1, 3)], [(2, 2)], [(2, 3), (3, 2)], [(3, 3)]],
        )
        load_pair_rows(2)
        load_w1_all(w1_late, 0, [[(4, 0), (4, 1)], [(4, 2), (4, 3)]])
        load_w1(w1_last_first, 0, [(5, 0), (5, 1)])
        load_w1(w1_late, 4, [(5, 2), (5, 3)])
        half_piece = {(s, h): piece[5, s][:, H * h : H * (h + 1)] for s in range(S) for h in range(2)}
        w2_rows = w2_words.rearrange("e s p n -> p (e s) n").bitcast(I32)

        def load_w2(first, last):
            tile = sbuf([P, 2 * N * (last - first)], U8, f"w2w{first}")
            nc.sync.dma_start(out=tile[:].bitcast(I32).rearrange("p (e n) -> p e n", e=last - first), in_=w2_rows[:, first:last, :])
            for e in range(first, last):
                w2w[e] = tile[:, 2 * N * (e - first) : 2 * N * (e - first + 1)]

        load_w2(0, EARLY)
        load_scale_rows(w2s, w2_scales.rearrange("e s q n -> (e s) q n"), N)
        load_w2(EARLY, E)

        def rounded_view(s, a, b):
            return rounded[s, 0][:, a:b, :] if b <= WIDE else rounded[s, 1][:, a - WIDE : b - WIDE, :]

        def cast(engine_copy, s, a, b):
            engine_copy(
                rounded_view(s, a, b).rearrange("p (c i) t -> p c t i", i=4),
                raw[s][:, :, a:b].rearrange("p t (c i) -> p c t i", i=4),
            )

        def quantise(s, a, b):
            nc.vector.quantize_mx(
                out=words[s][:, a:b].bitcast(E4M3), scales=scales[s][:, a:b], in_=rounded_view(s, a, b).rearrange("p c t -> p (c t)")
            )

        def round_and_quantise(s):
            cast(nc.scalar.copy, s, 0, WIDE)
            cast(nc.scalar.copy, s, WIDE, T)
            quantise(s, 0, WIDE)
            quantise(s, WIDE, T)

        slot_words = {}
        slot_scales = {}

        def gather_one(slots, tables, s, first, last, target):
            nc.vector.tensor_copy(target, tables[s][:].indirect(offsets[:, C * first // 16 : C * last // 16]))
            for e in range(first, last):
                slots[s, e] = target[:, C * (e - first) : C * (e - first + 1)]

        def gather(s, first, last, word_tile=None, scale_tile=None):
            width = C * (last - first)
            if word_tile is None:
                word_tile = sbuf([P, width], U32, f"slot_words{s}{first}")[:]
                scale_tile = sbuf([P, width], U8, f"slot_scales{s}{first}")[:]
            gather_one(slot_words, words, s, first, last, word_tile)
            gather_one(slot_scales, scales, s, first, last, scale_tile)

        for j in range(2):
            for engine_copy, a, b in ((nc.vector.tensor_copy, 0, SHARE), (nc.scalar.copy, WIDE, T), (nc.scalar.copy, SHARE, WIDE)):
                engine_copy(
                    rounded_view(0, a, b)[:, :, 2 * j : 2 * j + 2].rearrange("p (c i) t -> p c t i", i=4),
                    first_rows[j][:, :, a:b].rearrange("p t (c i) -> p c t i", i=4),
                )
        quantise(0, WIDE, T)
        quantise(0, 0, WIDE)
        gather(0, 0, E)
        round_and_quantise(1)
        gather(1, 0, EARLY)
        round_and_quantise(2)
        gather_one(slot_words, words, 2, 0, EARLY, sbuf([P, EARLY * C], U32, "slot_words20")[:])
        gather_one(slot_scales, scales, 2, 0, 2, sbuf([P, 2 * C], U8, "slot_scales20")[:])
        round_and_quantise(LAST)
        gather_one(slot_scales, scales, 2, 2, EARLY, sbuf([P, 2 * C], U8, "slot_scales22", "raw3")[:])

        late = C * (E - EARLY)
        word_pair = sbuf([P, 2 * late], U32, "word_pair", "rounded3a")
        scale_pair = sbuf([P, 2 * late], U8, "scale_pair", "rounded3b")
        gather(LAST, 0, 2)
        gather(LAST, 2, EARLY)
        gather(1, EARLY, E, word_pair[:, 0:late], scale_pair[:, 0:late])
        gather_one(slot_scales, scales, 2, EARLY, E, scale_pair[:, late:])
        gather_one(slot_words, words, 2, 4, 5, word_pair[:, late : late + C])
        gather_one(slot_words, words, LAST, 4, 5, sbuf([P, C], U32, "slot_words34")[:])
        gather_one(slot_scales, scales, LAST, EARLY, E, sbuf([P, late], U8, "slot_scales34")[:])
        gather_one(slot_words, words, 2, 5, 6, word_pair[:, late + C :])
        gather_one(slot_words, words, LAST, 5, 6, sbuf([P, C], U32, "slot_words35")[:])

        def first_layer(e, s):
            plane, u = planes[e // 2], e % 2
            nc.tensor.matmul_mx(
                out=bank[e][:],
                lhsT=slot_words[s, e].bitcast(E4M3),
                lhsT_scale=slot_scales[s, e],
                rhs=piece[e, s].bitcast(E2M1),
                rhs_scale=plane[:, H * (S * u + s) : H * (S * u + s + 1)],
                start=(s == 0),
                stop=(s == LAST),
            )
            if s == LAST:
                nc.scalar.activation(
                    hidden[e][:].rearrange("r (half p d) -> r half p d", half=2, d=2),
                    bank[e][:].rearrange("r (p half d) -> r half p d", half=2, d=2),
                    GELU,
                )

        def last_expert_half(h, s, target):
            nc.tensor.matmul_mx(
                out=target[:, 0 : H // 2],
                lhsT=slot_words[s, 5].bitcast(E4M3),
                lhsT_scale=slot_scales[s, 5],
                rhs=half_piece[s, h].bitcast(E2M1),
                rhs_scale=planes[2][:, H * (S + s) + H // 2 * h : H * (S + s) + H // 2 * (h + 1)],
                start=(s == 0),
                stop=(s == LAST),
            )
            if s == LAST:
                nc.scalar.activation(
                    hidden[5][:].rearrange("r (half p d) -> r half p d", half=2, d=2)[:, :, P // 2 * h : P // 2 * (h + 1), :],
                    target[:, 0 : H // 2].rearrange("r (p half d) -> r half p d", half=2, d=2),
                    GELU,
                )

        def turn(e, target, identity):
            pairs = hidden[e][:].bitcast(F32)
            for half in range(2):
                nc.tensor.transpose(target[:, C * half : C * (half + 1)], pairs[:, P * half : P * (half + 1)], identity[:])

        def copy_turned(engine_copy, hturned, source):
            engine_copy(
                hturned.bitcast(F32).rearrange("p (e c half) -> p e c half", c=C, half=2),
                source.rearrange("p (e half c) -> p e c half", c=C, half=2),
            )

        hwords = {}
        hscales = {}

        def quantise_h(first, last, hturned):
            word_tile = sbuf([P, C * (last - first)], U32, f"hwords{first}")
            scale_tile = sbuf([P, C * (last - first)], U8, f"hscales{first}")
            nc.vector.quantize_mx(out=word_tile[:].bitcast(E4M3), scales=scale_tile[:], in_=hturned)
            for e in range(first, last):
                hwords[e] = word_tile[:, C * (e - first) : C * (e - first + 1)]
                hscales[e] = scale_tile[:, C * (e - first) : C * (e - first + 1)]

        def second_layer(v, first, last, target):
            for e in range(first, last):
                nc.tensor.matmul_mx(
                    out=target[:, C * (e - first) : C * (e - first + 1)],
                    lhsT=w2w[e][:, 2 * P * v : 2 * P * (v + 1)].bitcast(E2M1),
                    lhsT_scale=w2s[:, N * e + P * v : N * e + P * (v + 1)],
                    rhs=hwords[e].bitcast(E4M3),
                    rhs_scale=hscales[e],
                    start=True,
                    stop=True,
                )
            (nc.scalar.copy, nc.vector.tensor_copy)[v](
                result[:, v, :, first:last, :],
                target[:, 0 : C * (last - first)].rearrange("p (e m u) -> p m e u", e=last - first, m=R),
            )

        for e, s in piece:
            if e < EARLY:
                first_layer(e, s)

        hturned_early = sbuf([P, EARLY * H], BF16, "hturned_early")
        turn(0, bank[2][:, 0 : 2 * C], ident)
        turn(1, bank[2][:, 2 * C : 4 * C], ident)
        turn(2, bank[1][:, 0 : 2 * C], ident)
        turn(3, bank[3][:, 0 : 2 * C], ident)
        copy_turned(nc.scalar.copy, hturned_early[:, 0 : 2 * H], bank[2][:])
        copy_turned(nc.scalar.copy, hturned_early[:, 2 * H : 3 * H], bank[1][:, 0 : 2 * C])
        copy_turned(nc.scalar.copy, hturned_early[:, 3 * H : 4 * H], bank[3][:, 0 : 2 * C])

        for s in range(S):
            first_layer(4, s)
        halves = (bank[5], bank[0])
        for h, s in [(h, s) for s in range(2) for h in range(2)] + [(h, s) for h in range(2) for s in (2, LAST)]:
            last_expert_half(h, s, halves[h])
        quantise_h(0, EARLY, hturned_early[:])

        hturned = {e: sbuf([P, H], BF16, f"hturned{e}") for e in (4, 5)}
        ident_end = placed.tile([P, P], F32, name="ident_end", offset=0, align_bytes=256)
        nc.vector.tensor_copy(ident_end[:], ident[:])
        for e, identity, engine_copy in ((4, ident_end, nc.vector.tensor_copy), (5, ident, nc.scalar.copy)):
            turn(e, bank[e][:, 0 : 2 * C], identity)
            copy_turned(engine_copy, hturned[e][:], bank[e][:, 0 : 2 * C])
            quantise_h(e, e + 1, hturned[e][:])

        for v, first, last, b in ((0, 0, 2, 6), (0, 2, 4, 7), (1, 0, 2, 1), (1, 2, 4, 2), (0, 4, 5, 3), (1, 4, 5, 4), (0, 5, 6, 0), (1, 5, 6, 5)):
            second_layer(v, first, last, bank[b])

        rows_out = out.rearrange("(v p) (m c) -> v p m c", v=2, m=R)
        for first, last in ((0, EARLY), (EARLY, E)):
            nc.sync.dma_start(
                out=rows_out[0][:, :, U * first : U * last], in_=result[:, 0, :, first:last, :].rearrange("p m e u -> p m (e u)")
            )
        nc.sync.dma_start(out=out[P:, :], in_=result[:, 1, :, :, :].rearrange("p m e u -> p (m e u)"))
